import numpy as np, ml_dtypes
CORES = [5,29,101,125,133,157,229,253]
N = 8
BF = ml_dtypes.bfloat16
CAP, S, Q, M, W, RO = 48, 384, 4, 6, 4096, 3
def blocks(m):
    return np.stack([m[:, 16 * g:16 * g + 16, 16 * g:16 * g + 16] for g in range(8)], axis=1)
def diag(m):
    z = np.zeros((N, 8, 16, 8, 16), m.dtype)
    for g in range(8): z[:, g, :, g, :] = m[:, g]
    return z.reshape(N, 128, 128)
def play(b, lu, pb, ob):
    live = b[:, :, 0, :] >= 0
    num = np.maximum(np.matmul(pb.swapaxes(2, 3), b), 0)
    h = np.zeros(b.shape, np.int64)
    for j in range(16): h = h + np.take_along_axis(lu, num[:, :, j:j + 1, :], axis=3)
    fire = (np.matmul(ob.swapaxes(2, 3), np.maximum(h, 0)) > 0) & live[:, :, None, :]
    b = np.where(fire, (b + 1) & (Q - 1), b)
    return b, np.where(live, np.add.reduce(b, axis=2) & (N - 1), -1)
def parts(rng):
    cells = np.argsort(rng.random((N, 8, 16, 16)), axis=-1)[..., :M]
    pb = np.zeros((N, 8, 16, 16), np.int64); np.put_along_axis(pb, cells, np.broadcast_to(Q ** np.arange(M), cells.shape), axis=-1)
    lu = np.clip(rng.integers(-127, 128, (N, 8, 16, W)) + rng.integers(-16, 17, (N, 8, 16, 1)), -127, 127)
    return np.ascontiguousarray(pb.swapaxes(2, 3)), lu, rng.integers(-1, 2, (N, 8, 16, 16))
def boards(rng, m):
    return np.where(m[:, :, None, :], rng.integers(0, Q, (N, 8, 16, S)), -1)
def pack(b, lu, pb, ob):
    w = lambda a: np.ascontiguousarray(a).astype(np.float32).astype(BF)
    return {"x": w(b.reshape(N, 128, S)), "lut": w(lu.reshape(N, 128, W)), "pl": w(diag(pb)), "pol": w(diag(ob))}
def setup_inputs(rng):
    pb, lu, ob = parts(rng); fill = rng.choice(np.array([0.6, 0.75, 0.9, 1.0]), (N, 8, 1))
    return pack(boards(rng, rng.random((N, 8, S)) < fill), lu, pb, ob)
def setup_inputs_room(rng):
    pb, lu, ob = parts(rng); lu[:, 7] = -np.abs(lu[:, 7]); pool = rng.integers(0, Q, (N, 8, 16, 3 * S)); to = play(pool, lu, pb, ob)[1]
    b = np.full((N, 8, 16, S), -1, np.int64)
    for a in range(N):
        for g in range(7):
            seq = rng.permutation(N); left = S; ix = [np.zeros(0, np.int64)]
            if a == 0: seq = np.concatenate([np.array([1]), seq[seq != 1]])
            for i in range(N):
                n = int(rng.choice(np.array([0, 1, CAP - 1, CAP, CAP + 1, 2 * CAP])))
                if a == 0 and i == 0: n = (CAP, CAP + 1, 2 * CAP, CAP - 1, 1, 0, CAP)[g]
                if g == 6: n = CAP
                n = min(n, left); left -= n
                if n > 0: ix.append(np.resize(np.flatnonzero(to[a, g] == seq[i]), n).astype(np.int64))
            ix = rng.permutation(np.concatenate(ix)); pos = rng.permutation(S)[:len(ix)]
            b[a, g][:, pos] = pool[a, g][:, ix]
        e = 2 * int(rng.integers(0, N // 2))
        if a == 0: e = 2
        if e == a: e = (a + 2) % N
        some = rng.integers(0, Q, (16, 16 * S)); s = np.add.reduce(some, axis=0) & (N - 1)
        b[a, 7] = some[:, np.concatenate([np.flatnonzero(s == e)[:270], np.flatnonzero(s == e + 1)[:S - 270]])]
    return pack(b, lu, pb, ob)
def setup_inputs_ties(rng):
    pb, lu, ob = parts(rng)
    lu[:, :2] = rng.integers(-1, 2, (N, 2, 16, W)); lu[:, 2] = rng.choice(np.array([-127, 127]), (N, 16, W)); ob[:, 2] = rng.choice(np.array([-1, 1]), (N, 16, 16))
    lu[:, 3] = lu[:, 3, :1]; lu[:, 4] = -np.abs(lu[:, 4]); lu[:, 5] = 127; ob[:, 5] = 1; ob[:, 5, :, 8:] = -1
    ob[:, 6, :, :4] = 0; ob[:, 6, :, 4:8] = -1; ob[:, 6, :, 8:12] = 1
    lu[:, 7] = np.abs(lu[:, 7]); lu[:, 7, 8:] = lu[:, 7, :8]; ob[:, 7, :8, :8] = 1; ob[:, 7, 8:, :8] = -1
    fill = rng.choice(np.array([0.7, 0.9, 1.0]), (N, 8, 1))
    b = boards(rng, rng.random((N, 8, S)) < fill)
    b[:, 4, :, 0] = 0; b[:, 4, :, 1:Q + 1] = Q - 1; b[:, 4, 15, 1:Q + 1] = np.arange(Q)
    b[:, 5, :8, 0] = Q - 1; b[:, 5, 8:, 0] = 0; b[:, 5, :8, 1] = Q - 2; b[:, 5, 8:, 1] = Q - 1
    return pack(b, lu, pb, ob)
def setup_inputs_alike(rng):
    pb, lu, ob = parts(rng); m = rng.random((N, 8, S)) < rng.choice(np.array([0.75, 0.95]), (N, 8, 1)); m[:, :3] = True
    b = boards(rng, m)
    b[:, 0] = b[:, 0, :, :1]; b[:, 1] = np.tile(b[:, 1, :, :2], (1, 1, S // 2)); b[:, 2] = (Q - 1) * rng.integers(0, 2, (N, 1, S))
    pb[:, 4] = pb[:, 4, :, :1]
    return pack(b, lu, pb, ob)
def setup_inputs_thin(rng):
    pb, lu, ob = parts(rng); q = rng.permutation(N); fill = np.zeros((N, 8, 1))
    fill[:, 4:, 0] = np.stack([rng.permutation(np.array([0.1, 0.4, 0.7, 1.0])) for i in range(N)])
    fill[:, 7, 0] = 0.9; fill[q[0]] = 0.0; fill[q[1], 2] = 1.0
    m = rng.random((N, 8, S)) < fill; m[:, 0, S - 1] = True; m[:, 1, 0] = True
    return pack(boards(rng, m), lu, pb, ob)
def setup_inputs_spread(rng):
    pb, lu, ob = parts(rng)
    lu = ((2 * rng.random((N, 8, 16, W)) - 1) * np.exp2(7 * rng.random((N, 8, 1, W)))).astype(np.int64) * (rng.random((N, 8, 1, W)) > 0.0625)
    m = rng.random((N, 8, 1, S)) < rng.choice(np.array([0.3, 0.8, 1.0]), (N, 8, 1, 1))
    v = np.minimum((Q * rng.random((N, 8, 16, S)) ** np.exp2(rng.integers(-2, 3, (N, 8, 16, 1)))).astype(np.int64), Q - 1)
    return pack(np.where(m, v, -1), lu, pb, ob)
def check_inputs(d):
    bad = []; v = {k: np.asarray(d[k]).astype(np.float32) for k in ("x", "lut", "pl", "pol")}
    for k, lo, hi in (("x", -1, Q - 1), ("lut", -127, 127), ("pol", -1, 1)):
        if not np.all((v[k] >= lo) & (v[k] <= hi) & (v[k] == np.floor(v[k]))): bad.append("range of " + k)
    e = v["x"].reshape(N, 8, 16, S) == -1
    if np.any(np.any(e, axis=2) != np.all(e, axis=2)): bad.append("empty slots of x")
    for k in ("pl", "pol"):
        if not np.all(diag(blocks(v[k])) == v[k]): bad.append("zeros outside the blocks of " + k)
    want = np.concatenate([np.zeros(16 - M), Q ** np.arange(M)])
    if not np.all(np.sort(blocks(v["pl"]), axis=2) == want[:, None]): bad.append("weights of pl")
    return bad
def reference(x, lut, pl, pol):
    whole = lambda a: a.astype(np.float32).astype(np.int64)
    b = whole(x).reshape(N, 8, 16, S); lu = whole(lut).reshape(N, 8, 16, W); pb = blocks(whole(pl)); ob = blocks(whole(pol))
    for ply in range(RO):
        b, to = play(b, lu, pb, ob)
        come = np.full((N, 8, 16, S), -1, np.int64)
        for a in range(N):
            for r in range(N):
                for g in range(8):
                    ix = np.flatnonzero(to[a, g] == r)[:CAP]
                    come[r, g, :, a * CAP:a * CAP + len(ix)] = b[a, g][:, ix]
        b = come
    return {"y": b.reshape(N, 128, S).astype(np.float32).astype(BF)}

@@ -1,0 +1,498 @@
+from concourse.bass import DstId, RemoteDMATransfer
+from concourse.mybir import AluOpType as ALU, ActivationFunctionType as ACT
+
+N, S, CAP, W, RO = 8, 384, 48, 4096, 3
+K = 136
+EMPTY = -1024.0
+STRIDE = S
+WIN = (N + 2) * STRIDE
+MID = WIN // 2
+BIG = 32768.0
+WSUM = 1365
+
+SCRATCH = {"lutb": ("sbuf", [128, W], "bfloat16"), "gat": ("sbuf", [128, 16 * S], "bfloat16"),
+           "pol16": ("sbuf", [128, 128], "float16"), "wd": ("sbuf", [128, 144], "float16"),
+           "init": ("sbuf", [128, 4], "float32"), "xm": ("sbuf", [128, S], "float32"),
+           "num16": ("sbuf", [128, S], "uint16"), "pos16": ("sbuf", [128, S // 16], "uint16"),
+           "r16": ("sbuf", [128, S], "float16"), "cum": ("sbuf", [128, S], "float32"), "val": ("sbuf", [128, S], "float16")}
+for _n in ("xb", "xs", "zero", "tt", "t0", "ee", "qq"):
+    SCRATCH[_n] = ("sbuf", [128, S], "bfloat16")
+for _n in ("plb", "polb", "ones", "ident", "shift", "ibig", "blk0", "corner", "bt0", "bt", "colt", "colm", "dd", "rrow"):
+    SCRATCH[_n] = ("sbuf", [128, 128], "bfloat16")
+for _n in ("wd0", "wd1", "wd2"):
+    SCRATCH[_n] = ("sbuf", [128, 144], "bfloat16")
+for _t in range(RO + 1):
+    SCRATCH["brd%d" % _t] = ("sbuf", [128, S], "bfloat16")
+for _t in range(RO):
+    SCRATCH["win%d" % _t] = ("sbuf", [128, WIN], "bfloat16")
+    SCRATCH["hand%d" % _t] = ("sbuf", [128, CAP], "bfloat16")
+BANKS = tuple("bank%d" % _b for _b in range(8))
+for _n in BANKS:
+    SCRATCH[_n] = ("psum", [128, 512], "float32")
+
+SEMAPHORES = ["cv", "cs", "cp", "cg", "ldx", "ldpl", "ldlut", "ldpol", "sty", "left"]
+for _t in range(RO):
+    SEMAPHORES += ["soon%d" % _t, "dir%d" % _t, "far%d" % _t, "hop%d" % _t]
+
+PLAN = {
+    "first": {"conv": [48, 336],
+              "gat": [("V", 40), ("S", 40), ("S", 72), ("V", 72), ("V", 56), ("S", 48), ("S", 40), ("V", 16)],
+              "h": [(112, "V"), (112, "V"), (96, "S"), (64, "S")],
+              "tail": [(160, "V", "V"), (128, "V", "S"), (96, "V", "S")],
+              "bias": {"scat": -600.0, "conv": -100.0, "relu": 600.0, "h": -300.0, "num": 300.0, "z": 100.0, "val": -300.0,
+                       "scan": 600.0}},
+    "later": {"perm": [0, 1, 3, 2, 4, 5, 7, 6], "conv": [48, 48, 48, 48, 48, 144],
+              "gat": [("V", 48), ("V", 24), ("S", 24), ("S", 32), ("V", 16), ("V", 40), ("S", 56), ("V", 48), ("S", 32),
+                      ("S", 40), ("V", 24)],
+              "h": [(48, "S"), (96, "V"), (96, "V"), (80, "S"), (64, "V")],
+              "tail": [(160, "V", "S"), (224, "V", "V")],
+              "bias": {"scat": -600.0, "scan": 300.0, "z": -100.0, "val": 300.0, "conv": 600.0, "relu": 100.0, "gat": -300.0,
+                       "wrap": 300.0, "h": -100.0, "q": 600.0, "t": 600.0}},
+    "look": 30.0,
+    "banks": {"pn": [0, 1], "ph": [2, 3, 4], "pw": [5], "pu": [6], "pc": [7], "po": [0]},
+}
+HELPERS_FIRST = (0, 1, 2)
+COST = {"f": 1.25, "gam": 1.56, "sig": 3.8, "pe": 0.42, "sem": 60.0, "load": 5500.0, "small": 2500.0,
+        "soon": 4200.0, "dir": 5200.0, "far": 5700.0}
+
+
+def routes(T, topo, a):
+    src = T.cores[a]
+    ring = [(a + k) % N for k in range(1, N)]
+    direct = [r for r in ring if topo.may_write(src, T.cores[r])]
+    far = [r for r in ring if r not in direct]
+    helpers = [c for c in topo.cores_of(src) if T.rank_of(c) is None and all(topo.may_write(c, T.cores[r]) for r in far)]
+    return direct, list(zip(helpers, far))
+
+
+def shares(engines, n):
+    sizes = [1] * n
+    while sum(sizes) + min(sizes) <= len(engines):
+        sizes[sizes.index(min(sizes))] *= 2
+    out, p = [], 0
+    for s in sorted(sizes, reverse=True):
+        out.append((sum(1 << e for e in engines[p:p + s]), s))
+        p += s
+    return out
+
+
+def masks(T, topo, a, t):
+    src = T.cores[a]
+    direct, hands = routes(T, topo, a)
+    off = topo.engines(src, T.cores[direct[0]])
+    on = topo.engines(src, hands[0][0])
+    if t not in HELPERS_FIRST:
+        on = [e for e in on if e not in off]
+    hm = [shares(topo.engines(h, T.cores[r]), 1)[0] for h, r in hands]
+    return shares(off, len(direct)), shares(on, len(hands)), hm
+
+
+def arrivals(T, topo, me):
+    way = {"soon": [0, []], "dir": [0, []], "far": [0, []]}
+    for a in range(N):
+        if a == me:
+            continue
+        direct, hands = routes(T, topo, a)
+        dm, _, hm = masks(T, topo, a, 0)
+        if me in direct:
+            k = direct.index(me)
+            w, n = ("soon" if k == 0 else "dir"), dm[k][1]
+        else:
+            w, n = "far", hm[[r for h, r in hands].index(me)][1]
+        way[w][0] += n
+        way[w][1].append(a)
+    return way
+
+
+def runs(sizes):
+    out, p = [], 0
+    for n in sizes:
+        out.append((p, p + n))
+        p += n
+    return out
+
+
+def make_ops(g, core, T, topo, me, plan):
+    ops = []
+    bias = {}
+    V, A, P = g.vector, g.scalar, g.tensor
+
+    def op(eng, fn, reads=(), writes=(), cost=("c", 64), ext=(), tag="", join=False, own=None):
+        ops.append({"eng": eng, "fn": fn, "r": [whole(a) for a in reads], "w": [whole(a) for a in writes], "cost": cost,
+                    "ext": list(ext), "tag": tag, "join": join, "own": own, "bias": bias.get(tag.rstrip("0123456789_"), 0.0)})
+
+    def whole(a):
+        return (a, 0, 1 << 20) if isinstance(a, str) else a
+
+    def ts(out, in0, s1, s2, o0, o1=None):
+        if o1 is None:
+            return [V.tensor_scalar(out, in0, s1, None, o0)]
+        return [V.tensor_scalar(out, in0, s1, s2, o0, o1)]
+
+    def fill(name, value, cols=slice(None), n=64):
+        op("V", lambda: [V.memset(T[name][:, cols], value)], [], [name], ("c", n))
+
+    def select(out, src, pattern, cmp, base, cm, n=128):
+        op("G", lambda: [g.affine_select(T[out][:, 0:n], T[src][:, 0:n], pattern, cmp, 0.0, base, cm)], [src], [out], ("g", n))
+
+    def both(out, a, b, o, n=256):
+        op("V", lambda: [V.tensor_tensor(T[out][:], T[a][:], T[b][:], o)], [a, b], [out], ("c", n))
+
+    def scal(out, src, scale=1.0, add=0.0, n=128):
+        op("S", lambda: [A.activation(T[out][:], T[src][:], ACT.Identity, add, scale)], [src], [out], ("c", n))
+
+    op("S", lambda: [A.dma_start(T.xb[:], T.x[:])], [], ["xb"], ("d", "small"), own="ldx")
+    op("Y", lambda: [g.sync.dma_start(T.plb[:], T.pl[:])], [], ["plb"], ("d", "small"), own="ldpl")
+    op("Y", lambda: [g.sync.dma_start(T.lutb[:], T.lut[:])], ["plb?"], ["lutb"], ("d", "load"), own="ldlut")
+    op("Y", lambda: [g.sync.dma_start(T.polb[:], T.pol[:])], [], ["polb"], ("d", "load"), own="ldpol")
+    ops[2]["behind"] = 1
+    ops[3]["behind"] = 2
+
+    op("G", lambda: [g.iota(T.rrow[:], [[0, 8], [1, 16]], 0, 0, allow_small_or_imprecise_dtypes=True)], [], ["rrow"], ("g", 128))
+    fill("ones", 1.0)
+    fill("wd0", 0.0)
+    fill("wd0", 1.0, slice(15, 144, 16))
+    fill("zero", 0.0, n=192)
+    select("ident", "ones", [[-1, 128]], ALU.is_equal, 0, 1)
+    select("shift", "ones", [[-1, 128]], ALU.is_equal, -1, 1)
+    op("V", lambda: ts(T.colt[:], T.rrow[:], float(N), 0.125, ALU.is_le, ALU.mult), ["rrow"], ["colt"])
+    fill("colt", -41.0 / 2 ** 18, slice(N + 1, 128, 16))
+    op("V", lambda: ts(T.colm[:], T.rrow[:], float(N), -1.0, ALU.is_le, ALU.mult), ["rrow"], ["colm"])
+    select("blk0", "colt", [[-16, 8], [0, 16]], ALU.is_ge, 0, 1)
+    select("bt0", "blk0", [[16, 8], [0, 16]], ALU.is_ge, 15, -1)
+    select("corner", "colm", [[-16, 8], [0, 16]], ALU.is_equal, 0, 1)
+    select("wd1", "wd0", [[1, 144]], ALU.is_ge, 0, -1, 144)
+    select("wd2", "wd1", [[-1, 144]], ALU.is_ge, 15, 1, 144)
+    op("P", lambda: [P.matmul(T.bank7[:, 0:1], T.rrow[0:1, :], T.ones[0:1, 0:1], True, True)], ["rrow", "ones"], [("bank7", 0, 1)],
+       ("p", 64))
+    op("V", lambda: ts(T.init[:, 0:1], T.bank7[:, 0:1], float(STRIDE), float(-1 - MID), ALU.mult, ALU.add), [("bank7", 0, 1)], ["init"])
+    op("V", lambda: ts(T.init[:, 1:2], T.bank7[:, 0:1], -0.125, -0.4375, ALU.mult, ALU.add), [("bank7", 0, 1)], ["init"])
+    both("bt", "bt0", "corner", ALU.add)
+    both("dd", "ident", "shift", ALU.subtract)
+    fill("dd", 0.0, slice(N, 128, 16))
+    fill("dd", 0.0, slice(15, 128, 16))
+    scal("ibig", "ident", BIG)
+    scal("wd", "wd2", n=144)
+    scal("pol16", "polb")
+
+    op("V", lambda: ts(T.xm[:], T.xb[:], 0.0, EMPTY + 1 - K, ALU.is_lt, ALU.mult), ["xb"], ["xm"], ("c", 384))
+    scal("xs", "xb", 1.0, float(K), S)
+    both("brd0", "xm", "xs", ALU.add, 768)
+
+    for t in range(RO):
+        value = -1 if t == RO - 1 else int(EMPTY)
+        for r in range(N):
+            p = r * STRIDE
+            op("G", lambda t=t, p=p, value=value: [g.iota(T["win%d" % t][:, p:p + CAP], [[0, CAP]], value, 0,
+                                                          allow_small_or_imprecise_dtypes=True)],
+               ["wd2"], [("win%d" % t, p, p + CAP)], ("g", CAP))
+
+    direct, hands = routes(T, topo, me)
+    way = arrivals(T, topo, me)
+    use = {}
+
+    def bank(kind):
+        use[kind] = use.get(kind, -1) + 1
+        z = plan["banks"][kind]
+        return "bank%d" % z[use[kind] % len(z)]
+
+    def ply(t):
+        pl = plan["first"] if t == 0 else plan["later"]
+        order = list(range(N)) if t == 0 else [me] + way["soon"][1] + way["dir"][1] + way["far"][1]
+        order = [order[k] for k in pl.get("perm", range(N))]
+        bn, wn, nb = "brd%d" % t, "win%d" % t, "brd%d" % (t + 1)
+        B, Wn = T[bn], T[wn]
+        last = t == RO - 1
+        bias.clear()
+        bias.update(pl.get("bias", {}))
+
+        def column(s):
+            return order.index(s // CAP) * CAP + s % CAP
+
+        def conv(lo, hi):
+            bk = bank("pn")
+            blocks = [order[k] for k in range(lo // CAP, hi // CAP)]
+            spans = []
+            for i, a in enumerate(blocks):
+                if spans and spans[-1][1] + spans[-1][2] == a * CAP:
+                    spans[-1][2] += CAP
+                else:
+                    spans.append([i * CAP, a * CAP, CAP])
+            ext = [("%s%d" % (w, t - 1), way[w][0], w, t - 1) for w in way if t > 0 and any(a in way[w][1] for a in blocks)]
+            op("P", lambda: [P.matmul(T[bk][:, c:c + n], T.plb[:], B[:, s:s + n], True, True) for c, s, n in spans],
+               ["plb"] + [(bn, s, s + n) for c, s, n in spans], [(bk, 0, hi - lo)],
+               ("p", sum(max(64, n) for c, s, n in spans)), ext, "num%d" % t)
+            op("V", lambda: ts(T.num16[:, lo:hi], T[bk][:, 0:hi - lo], -float(K * WSUM), 0.0, ALU.add, ALU.max),
+               [(bk, 0, hi - lo)], [("num16", lo, hi)], ("c", hi - lo), tag="conv%d" % t)
+
+        def gather(eng, lo, hi):
+            def fn():
+                src = T.lutb[:, 0:W].indirect(T.num16[:, lo:hi])
+                if eng == "V":
+                    return [V.tensor_copy(T.gat[:, 16 * lo:16 * hi], src)]
+                return [A.activation(T.gat[:, 16 * lo:16 * hi], src, ACT.Copy)]
+            op(eng, fn, ["lutb", ("num16", lo, hi)], [("gat", lo, hi)], ("ga", 16 * (hi - lo)), tag="gat%d_%d" % (t, lo))
+
+        def hsum(lo, hi, eng):
+            bk = bank("ph")
+            n = hi - lo
+            for j0 in range(0, 16, 4):
+                def fn(j0=j0):
+                    out = [P.matmul(T[bk][:, 0:n], T.ident[:], T.gat[:, 16 * lo + j:16 * hi:16], j == 0, j == 15)
+                           for j in range(j0, j0 + 4)]
+                    return out[-1:] if j0 == 12 else []
+                op("P", fn, ["ident", ("gat", lo, hi)], [(bk, 0, n)], ("p", 4 * max(64, n)), tag="h%d_%d" % (t, lo), join=j0 > 0)
+            if eng == "V":
+                op("V", lambda: ts(T.r16[:, lo:hi], T[bk][:, 0:n], 0.0, None, ALU.max), [(bk, 0, n)], [("r16", lo, hi)],
+                   ("c", n), tag="relu%d_%d" % (t, lo))
+            else:
+                op("S", lambda: [A.activation(T.r16[:, lo:hi], T[bk][:, 0:n], ACT.Relu)], [(bk, 0, n)], [("r16", lo, hi)],
+                   ("c", n), tag="relu%d_%d" % (t, lo))
+
+        def tail(lo, hi, et, eq):
+            n = hi - lo
+            pw, pu, pc, po = bank("pw"), bank("pu"), bank("pc"), bank("po")
+            spans = []
+            for s in range(lo, hi):
+                c = column(s)
+                if spans and spans[-1][2] + spans[-1][3] == c:
+                    spans[-1][3] += 1
+                else:
+                    spans.append([s - lo, s, c, 1])
+            for c0, s, c, m in sorted(spans, key=lambda z: z[2]):
+                def fn(c0=c0, s=s, c=c, m=m):
+                    P.matmul(T[pw][:, c0:c0 + m], T.ibig[:], B[:, s:s + m], True, False)
+                    return [P.matmul(T[pw][:, c0:c0 + m], T.pol16[:], T.r16[:, c:c + m], False, True)]
+                op("P", fn, ["ibig", "pol16", (bn, s, s + m), ("r16", c, c + m)], [(pw, c0, c0 + m)],
+                   ("p", max(64, m) * 2), tag="z%d_%d" % (t, s))
+            half = 0.5 - 0.5 / BIG
+            if et == "V":
+                op("V", lambda: ts(T.tt[:, lo:hi], T[pw][:, 0:n], 1.0 / BIG, half, ALU.mult, ALU.add),
+                   [(pw, 0, n)], [("tt", lo, hi)], ("c", n), tag="t%d_%d" % (t, lo))
+            else:
+                op("S", lambda: [A.activation(T.tt[:, lo:hi], T[pw][:, 0:n], ACT.Identity, half, 1.0 / BIG)],
+                   [(pw, 0, n)], [("tt", lo, hi)], ("c", n), tag="t%d_%d" % (t, lo))
+            op("V", lambda: ts(T.ee[:, lo:hi], T.tt[:, lo:hi], K + 4.0, -4.0, ALU.is_ge, ALU.mult),
+               [("tt", lo, hi)], [("ee", lo, hi)], ("c", n // 2), tag="e%d_%d" % (t, lo))
+
+            def fu():
+                P.matmul(T[pu][:, 0:n], T.bt[:], T.tt[:, lo:hi], True, False)
+                return []
+            op("P", fu, ["bt", ("tt", lo, hi)], [(pu, 0, n)], ("p", max(64, n)), tag="u%d_%d" % (t, lo))
+            op("P", lambda: [P.matmul(T[pu][:, 0:n], T.bt[:], T.ee[:, lo:hi], False, True)], [("ee", lo, hi)], [(pu, 0, n)],
+               ("p", max(64, n)), tag="ue%d_%d" % (t, lo), join=True)
+            if eq == "V":
+                op("V", lambda: ts(T.qq[:, lo:hi], T[pu][:, 0:n], T.init[:, 1:2], 0.0, ALU.add, ALU.max), ["init", (pu, 0, n)],
+                   [("qq", lo, hi)], ("c", n), tag="q%d_%d" % (t, lo))
+            else:
+                op("S", lambda: [A.activation(T.qq[:, lo:hi], T[pu][:, 0:n], ACT.Relu, T.init[:, 1:2], 1.0)], ["init", (pu, 0, n)],
+                   [("qq", lo, hi)], ("c", n), tag="q%d_%d" % (t, lo))
+            op("P", lambda: [P.matmul(T[pc][:, 0:n], T.dd[:], T.qq[:, lo:hi], True, True)], ["dd", ("qq", lo, hi)],
+               [(pc, 0, n)], ("p", max(64, n)), tag="ind%d_%d" % (t, lo))
+            if last:
+                op("S", lambda: [A.activation(T.t0[:, lo:hi], T.tt[:, lo:hi], ACT.Identity, -float(K), 1.0)],
+                   [("tt", lo, hi)], [("t0", lo, hi)], ("c", n), tag="tz_%d" % lo)
+            first = T.init[:, 0:1] if lo == 0 else T.cum[:, lo - 1:lo]
+            op("V", lambda: [V.tensor_tensor_scan(T.cum[:, lo:hi], T[pc][:, 0:n], T.zero[:, lo:hi], first, ALU.add, ALU.add)],
+               [(pc, 0, n), "zero", "init", ("cum", max(lo - 1, 0), lo)], [("cum", lo, hi)], ("c", n), tag="scan%d_%d" % (t, lo))
+            op("V", lambda: [V.tensor_tensor(T.val[:, lo:hi], T[pc][:, 0:n], T.cum[:, lo:hi], ALU.mult)],
+               [(pc, 0, n), ("cum", lo, hi)], [("val", lo, hi)], ("c", n), tag="val%d_%d" % (t, lo))
+            k = n // 16
+
+            def fw():
+                out = []
+                for i in range(16):
+                    out = [P.matmul(T[po][:, 0:k], T.wd[:, 15 - i:143 - i], T.val[:, lo + i:hi:16], i == 0, i == 15)]
+                return out
+            op("P", fw, ["wd", ("val", lo, hi)], [(po, 0, k)], ("p", 16 * 64), tag="wrap%d_%d" % (t, lo))
+            op("V", lambda: ts(T.pos16[:, lo // 16:hi // 16], T[po][:, 0:k], float(MID), None, ALU.add),
+               [(po, 0, k)], [("pos16", lo, hi)], ("c", k), tag="pos%d_%d" % (t, lo))
+            tb = "t0" if last else "tt"
+            op("V", lambda: [V.tensor_tensor(Wn[:, 0:WIN].indirect(T.pos16[:, lo // 16:hi // 16]), T[tb][:, lo:hi],
+                                             T.ee[:, lo:hi], ALU.add)],
+               [("pos16", lo, hi), (tb, lo, hi), ("ee", lo, hi)], [wn], ("sc", n), tag="scat%d_%d" % (t, lo))
+
+        for lo, hi in runs(pl["conv"]):
+            conv(lo, hi)
+        for (e, n), (lo, hi) in zip(pl["gat"], runs([n for e, n in pl["gat"]])):
+            gather(e, lo, hi)
+        tails = [z + (a, b) for (n, a, b), z in zip(pl["tail"], runs([n for n, a, b in pl["tail"]]))]
+        for (n, e), (lo, hi) in zip(pl["h"], runs([n for n, e in pl["h"]])):
+            hsum(lo, hi, e)
+            while tails and all(column(s) < hi for s in range(tails[0][0], tails[0][1])):
+                tail(*tails.pop(0))
+
+        dm, om, _ = masks(T, topo, me, t)
+
+        def send():
+            tr = []
+            for (h, r), (m, n) in zip(hands, om):
+                rid, pid = topo.addr(h, core)
+                tr.append(RemoteDMATransfer(dst_ids=[DstId(rid=rid, pnc=pid)], dma_engine_mask=m, remote_sem=T.sem["hop%d" % t],
+                                            src=Wn[:, r * STRIDE:r * STRIDE + CAP], dst=T["hand%d" % t][:]))
+            if t in HELPERS_FIRST:
+                g.remote_dma_fused(tr, local_sem=T.sem.left)
+                tr = []
+            for k, (r, (m, n)) in enumerate(zip(direct, dm)):
+                rid, pid = topo.addr(T.cores[r], core)
+                tr.append(RemoteDMATransfer(dst_ids=[DstId(rid=rid, pnc=pid)], dma_engine_mask=m,
+                                            remote_sem=T.sem[("dir%d" if k else "soon%d") % t],
+                                            src=Wn[:, r * STRIDE:r * STRIDE + CAP], dst=T[nb][:, me * CAP:(me + 1) * CAP]))
+            g.remote_dma_fused(tr, local_sem=T.sem.left)
+            return []
+        op("G", send, [wn], [], ("c", 500), tag="send%d" % t)
+        p = me * STRIDE
+        op("S", lambda: [A.activation(T[nb][:, me * CAP:(me + 1) * CAP], Wn[:, p:p + CAP], ACT.Copy)],
+           [(wn, p, p + CAP)], [(nb, me * CAP, (me + 1) * CAP)], ("c", 48), tag="own%d" % t)
+        return sum(n for m, n in dm + om)
+
+    left = sum([ply(t) for t in range(RO)])
+    op("Y", lambda: [g.sync.dma_start(T.y[:], T["brd%d" % RO][:])], ["brd%d" % RO], [], ("d", "small"),
+       [("%s%d" % (w, RO - 1), way[w][0], w, RO - 1) for w in way], "store", own="sty")
+    return ops, left
+
+
+def depend(ops):
+    seen = {}
+    for i, o in enumerate(ops):
+        dep = {}
+        acc = [(a, False) for a in o["r"]] + [(a, True) for a in o["w"]]
+        for a, isw in acc:
+            for j, (b, lo, hi), jw in seen.get(a[0], []):
+                meet = lo < a[2] and a[1] < hi and (isw or jw)
+                if ops[j]["eng"] != o["eng"]:
+                    if meet or b in BANKS:
+                        dep[j] = True
+                elif meet and not o["join"]:
+                    dep[j] = True
+                elif b in BANKS and o["eng"] == "P":
+                    dep.setdefault(j, False)
+        if "behind" in o:
+            dep.setdefault(o["behind"], False)
+        o["dep"] = dep
+        for a, isw in acc:
+            seen.setdefault(a[0], []).append((i, a, isw))
+
+
+def span(o, c):
+    kind, n = o["cost"]
+    if kind == "d":
+        return 100.0, c[n]
+    cyc = 0.83 * c["f"]
+    if kind == "p":
+        d = 12 + n * c["pe"] * c["f"]
+    elif kind == "c":
+        d = 40 + max(64, n) * cyc
+    else:
+        d = {"g": 170 + 2 * n * cyc, "ga": 60 + n * c["gam"] * cyc, "sc": 60 + n * c["sig"] * cyc}[kind]
+    return d, d
+
+
+def arrange(ops, c, look, fixed=None):
+    n = len(ops)
+    sent = {int(o["tag"][4:]): i for i, o in enumerate(ops) if o["tag"].startswith("send")}
+    sp = [span(o, c) for o in ops]
+    pre = [set(o["dep"]) | set(sent[e[3]] for e in o["ext"]) for o in ops]
+    post = [[] for o in ops]
+    for i in range(n):
+        for j in pre[i]:
+            post[j].append(i)
+    rank = [0.0] * n
+    for i in range(n - 1, -1, -1):
+        rank[i] += sp[i][1] + ops[i]["bias"]
+        for j in ops[i]["dep"]:
+            rank[j] = max(rank[j], rank[i] + c["sem"])
+        for e in ops[i]["ext"]:
+            rank[sent[e[3]]] = max(rank[sent[e[3]]], rank[i] + c[e[2]])
+    end, start, out = [None] * n, [None] * n, []
+    free = {e: 0.0 for e in "VSPGY"}
+    missing = [len(p) for p in pre]
+    ready = {i: 0.0 for i in range(n) if not pre[i]}
+    heads = None if fixed is None else {e: [i for i in fixed if ops[i]["eng"] == e] for e in free}
+    while ready:
+        pool = ready if heads is None else [q[0] for q in heads.values() if q and q[0] in ready]
+        cand = [(max(ready[i], free[ops[i]["eng"]]), i) for i in pool]
+        s0, i0 = min(cand)
+        s, i = max([z for z in cand if ops[z[1]]["eng"] == ops[i0]["eng"] and z[0] <= s0 + look], key=lambda z: rank[z[1]])
+        start[i], end[i] = s, s + sp[i][1]
+        free[ops[i]["eng"]] = s + sp[i][0]
+        out.append(i)
+        del ready[i]
+        if heads is not None:
+            heads[ops[i]["eng"]].pop(0)
+        for k in post[i]:
+            missing[k] -= 1
+            if not missing[k]:
+                o = ops[k]
+                ready[k] = max([end[j] + c["sem"] if wt else start[j] for j, wt in o["dep"].items()]
+                               + [start[sent[e[3]]] + c[e[2]] for e in o["ext"]])
+    return out, start, end
+
+
+def emit(g, T, ops, order, left):
+    queue = {"V": g.vector, "S": g.scalar, "P": g.tensor, "G": g, "Y": g.sync}
+    counter = {"V": "cv", "S": "cs", "P": "cp", "G": "cg"}
+    count = {}
+    mark = {}
+    know = {e: {} for e in queue}
+    after = {}
+    for i in order:
+        o = ops[i]
+        e = o["eng"]
+        need = {}
+        for j, wt in o["dep"].items():
+            if wt and j in mark:
+                s, v = mark[j]
+                need[s] = max(need.get(s, 0), v)
+        for x in o["ext"]:
+            need[x[0]] = x[1]
+        for s, v in sorted(need.items(), key=lambda z: -len(after.get(z, {}))):
+            if know[e].get(s, 0) < v:
+                queue[e].wait_ge(T.sem[s], v)
+                know[e][s] = v
+                for s2, v2 in after.get((s, v), {}).items():
+                    know[e][s2] = max(know[e].get(s2, 0), v2)
+        ins = o["fn"]()
+        if o["own"]:
+            ins[0].then_inc(T.sem[o["own"]], 16)
+            mark[i] = (o["own"], 16)
+            count[o["own"]] = 16
+        elif ins:
+            s = counter[e]
+            for z in ins:
+                z.then_inc(T.sem[s], 1)
+                count[s] = count.get(s, 0) + 1
+            mark[i] = (s, count[s])
+        if i in mark:
+            after[mark[i]] = dict(know[e])
+    for s, v in count.items():
+        if not any(k.get(s, 0) >= v for k in know.values()):
+            (g.sync if s == "sty" else g).wait_ge(T.sem[s], v)
+    g.wait_ge(T.sem.left, left)
+
+
+def helper_program(g, core, T, topo):
+    for a in range(N):
+        for i, (h, r) in enumerate(routes(T, topo, a)[1]):
+            if h != core:
+                continue
+            rid, pid = topo.addr(T.cores[r], core)
+            total = 0
+            for t in range(RO):
+                _, om, hm = masks(T, topo, a, t)
+                g.wait_ge(T.sem["hop%d" % t], om[i][1])
+                g.remote_dma(T["brd%d" % (t + 1)][:, a * CAP:(a + 1) * CAP], T["hand%d" % t][:], T.sem["far%d" % t], T.sem.left,
+                             pid, rid, hm[i][0])
+                total += hm[i][1]
+            g.wait_ge(T.sem.left, total)
+
+
+def rank_program(g, core, T, topo):
+    me = T.rank_of(core)
+    if me is None:
+        helper_program(g, core, T, topo)
+        return
+    ops, left = make_ops(g, core, T, topo, me, PLAN)
+    depend(ops)
+    order, _, _ = arrange(ops, COST, PLAN["look"])
+    emit(g, T, ops, order, left)

@@ -3,24 +3,23 @@ from concourse.mybir import AluOpType as ALU, ActivationFunctionType as ACT
 
 N, S, CAP, W, RO = 8, 384, 48, 4096, 3
 K = 136
-EMPTY = -1024.0
 STRIDE = S
-WIN = (N + 2) * STRIDE
-MID = WIN // 2
+SPARE = S + 16
+MID = N // 2 * STRIDE
+WIN = N * STRIDE + SPARE
 BIG = 32768.0
 WSUM = 1365
 
-SCRATCH = {"lutb": ("sbuf", [128, W], "bfloat16"), "gat": ("sbuf", [128, 16 * S], "bfloat16"),
-           "pol16": ("sbuf", [128, 128], "float16"), "wd": ("sbuf", [128, 144], "float16"),
-           "init": ("sbuf", [128, 4], "float32"), "xm": ("sbuf", [128, S], "float32"),
-           "num16": ("sbuf", [128, S], "uint16"), "pos16": ("sbuf", [128, S // 16], "uint16"),
-           "r16": ("sbuf", [128, S], "float16"), "cum": ("sbuf", [128, S], "float32"), "val": ("sbuf", [128, S], "float16")}
-for _n in ("xb", "xs", "zero", "tt", "t0", "ee", "qq"):
-    SCRATCH[_n] = ("sbuf", [128, S], "bfloat16")
-for _n in ("plb", "polb", "ones", "ident", "shift", "ibig", "blk0", "corner", "bt0", "bt", "colt", "colm", "dd", "rrow"):
+SCRATCH = {"pol16": ("sbuf", [128, 128], "float16"), "wd": ("sbuf", [128, 144], "float16"), "init": ("sbuf", [128, 4], "float32"),
+           "ddx": ("sbuf", [128, 144], "bfloat16"), "step": ("sbuf", [128, S // 2], "bfloat16"),
+           "rows": ("sbuf", [128, 392], "float32"), "mrow": ("sbuf", [128, 32], "bfloat16"), "wd0": ("sbuf", [128, 144], "bfloat16"),
+           "lutb": ("sbuf", [128, W], "bfloat16"), "gat": ("sbuf", [128, 16 * S], "bfloat16"), "qq": ("sbuf", [128, S + 16], "bfloat16"),
+           "pos": ("sbuf", [128, 48], "uint16")}
+for _n in ("plb", "polb", "ones", "ident", "ibig", "bt", "both"):
     SCRATCH[_n] = ("sbuf", [128, 128], "bfloat16")
-for _n in ("wd0", "wd1", "wd2"):
-    SCRATCH[_n] = ("sbuf", [128, 144], "bfloat16")
+for _n, _d in (("num", "uint16"), ("relu", "float16"), ("tt", "bfloat16"), ("ee", "bfloat16"), ("t0", "bfloat16"), ("cum", "float32"),
+               ("val", "float16"), ("xb", "bfloat16"), ("xm", "bfloat16")):
+    SCRATCH[_n] = ("sbuf", [128, S], _d)
 for _t in range(RO + 1):
     SCRATCH["brd%d" % _t] = ("sbuf", [128, S], "bfloat16")
 for _t in range(RO):
@@ -30,30 +29,15 @@ BANKS = tuple("bank%d" % _b for _b in range(8))
 for _n in BANKS:
     SCRATCH[_n] = ("psum", [128, 512], "float32")
 
-SEMAPHORES = ["cv", "cs", "cp", "cg", "ldx", "ldpl", "ldlut", "ldpol", "sty", "left"]
+SEMAPHORES = ["cv", "cs", "cp", "cg", "ldx", "ldpl", "ldpol", "ldlut", "sty", "left"]
 for _t in range(RO):
-    SEMAPHORES += ["soon%d" % _t, "dir%d" % _t, "far%d" % _t, "hop%d" % _t]
+    SEMAPHORES += ["%s%d" % (_w, _t) for _w in ("soon", "dir", "far", "hop")]
 
-PLAN = {
-    "first": {"conv": [48, 336],
-              "gat": [("V", 40), ("S", 40), ("S", 72), ("V", 72), ("V", 56), ("S", 48), ("S", 40), ("V", 16)],
-              "h": [(112, "V"), (112, "V"), (96, "S"), (64, "S")],
-              "tail": [(160, "V", "V"), (128, "V", "S"), (96, "V", "S")],
-              "bias": {"scat": -600.0, "conv": -100.0, "relu": 600.0, "h": -300.0, "num": 300.0, "z": 100.0, "val": -300.0,
-                       "scan": 600.0}},
-    "later": {"perm": [0, 1, 3, 2, 4, 5, 7, 6], "conv": [48, 48, 48, 48, 48, 144],
-              "gat": [("V", 48), ("V", 24), ("S", 24), ("S", 32), ("V", 16), ("V", 40), ("S", 56), ("V", 48), ("S", 32),
-                      ("S", 40), ("V", 24)],
-              "h": [(48, "S"), (96, "V"), (96, "V"), (80, "S"), (64, "V")],
-              "tail": [(160, "V", "S"), (224, "V", "V")],
-              "bias": {"scat": -600.0, "scan": 300.0, "z": -100.0, "val": 300.0, "conv": 600.0, "relu": 100.0, "gat": -300.0,
-                       "wrap": 300.0, "h": -100.0, "q": 600.0, "t": 600.0}},
-    "look": 30.0,
-    "banks": {"pn": [0, 1], "ph": [2, 3, 4], "pw": [5], "pu": [6], "pc": [7], "po": [0]},
-}
-HELPERS_FIRST = (0, 1, 2)
-COST = {"f": 1.25, "gam": 1.56, "sig": 3.8, "pe": 0.42, "sem": 60.0, "load": 5500.0, "small": 2500.0,
-        "soon": 4200.0, "dir": 5200.0, "far": 5700.0}
+PLAN = {"first": {"gat": 24, "conv": [4, 4], "h": [96, 96, 96, 48, 48], "front": [192, 96, 96], "back": [192, 96, 96]},
+        "later": {"gat": 24, "fargat": 24, "conv": [2, 2, 2], "h": [1, 3, 5], "front": [3, 5], "back": [3]},
+        "look": 0.0, "piece": 2}
+COST = {"f": 1.0, "gam": 1.56, "sig": 3.0, "pe": 0.42, "sem": 220.0, "load": 4200.0, "pol": 4600.0, "first": 1500.0,
+        "small": 1600.0, "soon": 1800.0, "dir": 3000.0, "far": 3000.0, "yield": 0.0}
 
 
 def routes(T, topo, a):
@@ -76,13 +60,11 @@ def shares(engines, n):
     return out
 
 
-def masks(T, topo, a, t):
+def masks(T, topo, a):
     src = T.cores[a]
     direct, hands = routes(T, topo, a)
     off = topo.engines(src, T.cores[direct[0]])
     on = topo.engines(src, hands[0][0])
-    if t not in HELPERS_FIRST:
-        on = [e for e in on if e not in off]
     hm = [shares(topo.engines(h, T.cores[r]), 1)[0] for h, r in hands]
     return shares(off, len(direct)), shares(on, len(hands)), hm
 
@@ -93,7 +75,7 @@ def arrivals(T, topo, me):
         if a == me:
             continue
         direct, hands = routes(T, topo, a)
-        dm, _, hm = masks(T, topo, a, 0)
+        dm, _, hm = masks(T, topo, a)
         if me in direct:
             k = direct.index(me)
             w, n = ("soon" if k == 0 else "dir"), dm[k][1]
@@ -104,22 +86,26 @@ def arrivals(T, topo, me):
     return way
 
 
-def runs(sizes):
-    out, p = [], 0
+def runs(sizes, p=0):
+    out = []
     for n in sizes:
         out.append((p, p + n))
         p += n
     return out
 
 
+def part(r):
+    return r * STRIDE + (SPARE if r * STRIDE >= MID else 0)
+
+
 def make_ops(g, core, T, topo, me, plan):
     ops = []
-    bias = {}
     V, A, P = g.vector, g.scalar, g.tensor
 
-    def op(eng, fn, reads=(), writes=(), cost=("c", 64), ext=(), tag="", join=False, own=None):
+    def op(eng, fn, reads=(), writes=(), cost=("c", 64), ext=(), tag="", join=False, own=None, behind=None):
         ops.append({"eng": eng, "fn": fn, "r": [whole(a) for a in reads], "w": [whole(a) for a in writes], "cost": cost,
-                    "ext": list(ext), "tag": tag, "join": join, "own": own, "bias": bias.get(tag.rstrip("0123456789_"), 0.0)})
+                    "ext": list(ext), "tag": tag, "join": join, "own": own, "behind": behind})
+        return len(ops) - 1
 
     def whole(a):
         return (a, 0, 1 << 20) if isinstance(a, str) else a
@@ -130,226 +116,217 @@ def make_ops(g, core, T, topo, me, plan):
         return [V.tensor_scalar(out, in0, s1, s2, o0, o1)]
 
     def fill(name, value, cols=slice(None), n=64):
-        op("V", lambda: [V.memset(T[name][:, cols], value)], [], [name], ("c", n))
+        op("V", lambda e: [V.memset(T[name][:, cols], value)], [], [name], ("c", n))
 
-    def select(out, src, pattern, cmp, base, cm, n=128):
-        op("G", lambda: [g.affine_select(T[out][:, 0:n], T[src][:, 0:n], pattern, cmp, 0.0, base, cm)], [src], [out], ("g", n))
+    def select(name, pattern, cmp, base, cm, cols=slice(0, 128), put=0.0):
+        op("G", lambda e: [g.affine_select(T[name][:, cols], T[name][:, cols], pattern, cmp, put, base, cm)], [name], [name],
+           ("g", cols.stop - cols.start))
 
-    def both(out, a, b, o, n=256):
-        op("V", lambda: [V.tensor_tensor(T[out][:], T[a][:], T[b][:], o)], [a, b], [out], ("c", n))
+    def count(out, pattern, base, name, n, reads=(), behind=None):
+        op("G", lambda e: [g.iota(out, pattern, base, 0, allow_small_or_imprecise_dtypes=True)], reads, [name], ("g", n),
+           behind=behind)
 
-    def scal(out, src, scale=1.0, add=0.0, n=128):
-        op("S", lambda: [A.activation(T[out][:], T[src][:], ACT.Identity, add, scale)], [src], [out], ("c", n))
+    def affine(out, src, scale, add, reads, writes, n, relu=False, tag="", eng="F"):
+        def fn(e):
+            if e == "S":
+                return [A.activation(out, src, ACT.Relu if relu else ACT.Identity, add, scale)]
+            if relu:
+                return ts(out, src, add, 0.0, ALU.add, ALU.max)
+            return ts(out, src, scale, add, ALU.mult, ALU.add)
+        op(eng, fn, reads, writes, ("c", n), tag=tag)
 
-    op("S", lambda: [A.dma_start(T.xb[:], T.x[:])], [], ["xb"], ("d", "small"), own="ldx")
-    op("Y", lambda: [g.sync.dma_start(T.plb[:], T.pl[:])], [], ["plb"], ("d", "small"), own="ldpl")
-    op("Y", lambda: [g.sync.dma_start(T.lutb[:], T.lut[:])], ["plb?"], ["lutb"], ("d", "load"), own="ldlut")
-    op("Y", lambda: [g.sync.dma_start(T.polb[:], T.pol[:])], [], ["polb"], ("d", "load"), own="ldpol")
-    ops[2]["behind"] = 1
-    ops[3]["behind"] = 2
+    def mm(steps, reads, writes, tag="", ext=(), start=True, stop=True):
+        def fn(e):
+            out = [P.matmul(o, l, r, start and i == 0, stop and i == len(steps) - 1) for i, (o, l, r, n) in enumerate(steps)]
+            return out[-1:] if stop else []
+        op("P", fn, reads, writes, ("p", sum(max(64, z[3]) for z in steps)), ext, tag, join=not start)
 
-    op("G", lambda: [g.iota(T.rrow[:], [[0, 8], [1, 16]], 0, 0, allow_small_or_imprecise_dtypes=True)], [], ["rrow"], ("g", 128))
+    def load(queue, name, src, cost, sem, behind=None):
+        q = {"S": A, "Y": g.sync}[queue]
+        return op(queue, lambda e: [q.dma_start(T[name][:], src[:])], [], [name], ("d", cost), own=sem, behind=behind)
+    load("S", "xb", T.x, "small", "ldx")
+    i = load("Y", "plb", T.pl, "small", "ldpl")
+    i = load("Y", "lutb", T.lut, "load", "ldlut", i)
+    load("Y", "polb", T.pol, "pol", "ldpol", i)
+
+    fill("ident", 1.0)
+    select("ident", [[-1, 128]], ALU.is_equal, 0, 1)
+    affine(T.ibig[:], T.ident[:], BIG, 0.0, ["ident"], ["ibig"], 128)
+    affine(T.pol16[:], T.polb[:], 1.0, 0.0, ["polb"], ["pol16"], 128)
+    fill("bt", 0.125)
+    select("bt", [[0, 8], [-1, 16]], ALU.is_ge, N, 0)
+    select("bt", [[-16, 8], [0, 16]], ALU.is_ge, 0, 1)
+    select("bt", [[16, 8], [0, 16]], ALU.is_ge, 15, -1)
     fill("ones", 1.0)
+    fill("rows", 1.0, slice(384, 392))
+    count(T.rows[0:1, 0:128], [[0, 8], [1, 16]], 0, ("rows", 0, 128), 128)
+    count(T.rows[0:1, 128:256], [[2, 8], [1, 16]], MID, ("rows", 128, 256), 128)
+    count(T.rows[0:1, 256:384], [[-1, 16], [MID + SPARE, 2], [STRIDE, N // 2]], 1 - MID, ("rows", 256, 384), 128)
+    count(T.mrow[0:1, :], [[16, 32]], 0, "mrow", 32)
+    for j in range(3):
+        mm([(T.bank7[:, j:j + 1], T.rows[0:1, 128 * j:128 * j + 128], T.rows[0:1, 384:385], 256)], ["rows"], [("bank7", j, j + 1)])
+    affine(T.init[:, 0:1], T.bank7[:, 0:1], -0.125, -K - 0.4375, ["bank7"], ["init"], 64)
+    affine(T.init[:, 1:3], T.bank7[:, 1:3], 1.0, 0.0, ["bank7"], ["init"], 64)
+    fill("step", -2.0)
+    fill("ddx", 0.0)
+    select("ddx", [[-1, 128]], ALU.not_equal, 0, 1, slice(8, 136), 1.0)
+    select("ddx", [[-1, 128]], ALU.not_equal, -1, 1, slice(8, 136), -1.0)
+    select("ddx", [[0, 8], [-1, 16]], ALU.is_ge, N - 1, 0, slice(8, 136))
+    same = [T.ddx[:, 8:136], T.ddx[:, 0:128]]
+    op("V", lambda e: [V.tensor_tensor(T.both[:], same[0], same[1], ALU.add)], ["ddx"], ["both"], ("c", 256))
+    earlier = [(T.both[:], 0), (same[1], 1), (same[0], -1)]
     fill("wd0", 0.0)
+    fill("wd0", 1.0, slice(14, 144, 16))
     fill("wd0", 1.0, slice(15, 144, 16))
-    fill("zero", 0.0, n=192)
-    select("ident", "ones", [[-1, 128]], ALU.is_equal, 0, 1)
-    select("shift", "ones", [[-1, 128]], ALU.is_equal, -1, 1)
-    op("V", lambda: ts(T.colt[:], T.rrow[:], float(N), 0.125, ALU.is_le, ALU.mult), ["rrow"], ["colt"])
-    fill("colt", -41.0 / 2 ** 18, slice(N + 1, 128, 16))
-    op("V", lambda: ts(T.colm[:], T.rrow[:], float(N), -1.0, ALU.is_le, ALU.mult), ["rrow"], ["colm"])
-    select("blk0", "colt", [[-16, 8], [0, 16]], ALU.is_ge, 0, 1)
-    select("bt0", "blk0", [[16, 8], [0, 16]], ALU.is_ge, 15, -1)
-    select("corner", "colm", [[-16, 8], [0, 16]], ALU.is_equal, 0, 1)
-    select("wd1", "wd0", [[1, 144]], ALU.is_ge, 0, -1, 144)
-    select("wd2", "wd1", [[-1, 144]], ALU.is_ge, 15, 1, 144)
-    op("P", lambda: [P.matmul(T.bank7[:, 0:1], T.rrow[0:1, :], T.ones[0:1, 0:1], True, True)], ["rrow", "ones"], [("bank7", 0, 1)],
-       ("p", 64))
-    op("V", lambda: ts(T.init[:, 0:1], T.bank7[:, 0:1], float(STRIDE), float(-1 - MID), ALU.mult, ALU.add), [("bank7", 0, 1)], ["init"])
-    op("V", lambda: ts(T.init[:, 1:2], T.bank7[:, 0:1], -0.125, -0.4375, ALU.mult, ALU.add), [("bank7", 0, 1)], ["init"])
-    both("bt", "bt0", "corner", ALU.add)
-    both("dd", "ident", "shift", ALU.subtract)
-    fill("dd", 0.0, slice(N, 128, 16))
-    fill("dd", 0.0, slice(15, 128, 16))
-    scal("ibig", "ident", BIG)
-    scal("wd", "wd2", n=144)
-    scal("pol16", "polb")
+    select("wd0", [[-16, 9], [-8, 16]], ALU.is_ge, 112, 1, slice(0, 144))
+    select("wd0", [[16, 9], [8, 16]], ALU.is_ge, 7 - 112, -1, slice(0, 144))
+    affine(T.wd[:], T.wd0[:], 1.0, 0.0, ["wd0"], ["wd"], 144)
+    fill("qq", 0.0, slice(0, 8))
 
-    op("V", lambda: ts(T.xm[:], T.xb[:], 0.0, EMPTY + 1 - K, ALU.is_lt, ALU.mult), ["xb"], ["xm"], ("c", 384))
-    scal("xs", "xb", 1.0, float(K), S)
-    both("brd0", "xm", "xs", ALU.add, 768)
+    op("V", lambda e: ts(T.xm[:], T.xb[:], 0.0, float(K), ALU.is_ge, ALU.mult), ["xb"], ["xm"], ("c", S // 2))
+    op("V", lambda e: [V.tensor_tensor(T.brd0[:], T.xm[:], T.xb[:], ALU.add)], ["xm", "xb"], ["brd0"], ("c", 2 * S))
 
-    for t in range(RO):
-        value = -1 if t == RO - 1 else int(EMPTY)
-        for r in range(N):
-            p = r * STRIDE
-            op("G", lambda t=t, p=p, value=value: [g.iota(T["win%d" % t][:, p:p + CAP], [[0, CAP]], value, 0,
-                                                          allow_small_or_imprecise_dtypes=True)],
-               ["wd2"], [("win%d" % t, p, p + CAP)], ("g", CAP))
+    def clear(t, behind):
+        wn = "win%d" % t
+        for p in map(part, range(N)):
+            count(T[wn][:, p:p + CAP], [[0, CAP]], -1 if t == RO - 1 else 0, (wn, p, p + CAP), CAP, ["wd0"], behind)
+    clear(0, None)
 
     direct, hands = routes(T, topo, me)
     way = arrivals(T, topo, me)
-    use = {}
-
-    def bank(kind):
-        use[kind] = use.get(kind, -1) + 1
-        z = plan["banks"][kind]
-        return "bank%d" % z[use[kind] % len(z)]
+    dm, om, _ = masks(T, topo, me)
 
     def ply(t):
         pl = plan["first"] if t == 0 else plan["later"]
-        order = list(range(N)) if t == 0 else [me] + way["soon"][1] + way["dir"][1] + way["far"][1]
-        order = [order[k] for k in pl.get("perm", range(N))]
+        last = t == RO - 1
         bn, wn, nb = "brd%d" % t, "win%d" % t, "brd%d" % (t + 1)
         B, Wn = T[bn], T[wn]
-        last = t == RO - 1
-        bias.clear()
-        bias.update(pl.get("bias", {}))
+        if t == 0:
+            lots = [(None, list(range(a, b))) for a, b in runs(pl["conv"])]
+        else:
+            late = sorted(way["far"][1] + way["dir"][1])
+            lots = [(None, [me]), ("soon", way["soon"][1])] + [("far", late[a:b]) for a, b in runs(pl["conv"])]
+            pl = dict(pl)
+            for z in ("h", "front", "back"):
+                cut = [0] + [CAP * late[k] for k in pl[z]] + [S]
+                pl[z] = [b - a for a, b in zip(cut, cut[1:]) if b > a]
 
-        def column(s):
-            return order.index(s // CAP) * CAP + s % CAP
+        def gather(c, k, n):
+            def fn(e):
+                src = T.lutb[:, 0:W].indirect(T.num[:, c:c + n])
+                if e == "V":
+                    return [V.tensor_copy(T.gat[:, 16 * k:16 * (k + n)], src)]
+                return [A.activation(T.gat[:, 16 * k:16 * (k + n)], src, ACT.Copy)]
+            op("F", fn, ["lutb", ("num", c, c + n)], [("gat", k, k + n)], ("ga", 16 * n), tag="gat%d_%d" % (t, k))
 
-        def conv(lo, hi):
-            bk = bank("pn")
-            blocks = [order[k] for k in range(lo // CAP, hi // CAP)]
+        def arrived(blocks):
+            return [("%s%d" % (w, t - 1), way[w][0], w, t - 1) for w in way if t > 0 and any(a in way[w][1] for a in blocks)]
+
+        col = 0
+        for i, (w, blocks) in enumerate(lots):
+            bk = BANKS[6 + i % 2]
             spans = []
-            for i, a in enumerate(blocks):
+            for j, a in enumerate(blocks):
                 if spans and spans[-1][1] + spans[-1][2] == a * CAP:
                     spans[-1][2] += CAP
                 else:
-                    spans.append([i * CAP, a * CAP, CAP])
-            ext = [("%s%d" % (w, t - 1), way[w][0], w, t - 1) for w in way if t > 0 and any(a in way[w][1] for a in blocks)]
-            op("P", lambda: [P.matmul(T[bk][:, c:c + n], T.plb[:], B[:, s:s + n], True, True) for c, s, n in spans],
-               ["plb"] + [(bn, s, s + n) for c, s, n in spans], [(bk, 0, hi - lo)],
-               ("p", sum(max(64, n) for c, s, n in spans)), ext, "num%d" % t)
-            op("V", lambda: ts(T.num16[:, lo:hi], T[bk][:, 0:hi - lo], -float(K * WSUM), 0.0, ALU.add, ALU.max),
-               [(bk, 0, hi - lo)], [("num16", lo, hi)], ("c", hi - lo), tag="conv%d" % t)
+                    spans.append([j * CAP, a * CAP, CAP])
+            n = CAP * len(blocks)
+            op("P", lambda e, bk=bk, spans=spans: [P.matmul(T[bk][:, c:c + m], T.plb[:], B[:, k:k + m], True, True)
+                                                   for c, k, m in spans][-1:],
+               ["plb"] + [(bn, k, k + m) for c, k, m in spans], [(bk, 0, n)], ("p", sum(max(64, m) for c, k, m in spans)),
+               arrived(blocks), "num%d" % t)
+            op("V", lambda e, bk=bk, col=col, n=n: ts(T.num[:, col:col + n], T[bk][:, 0:n], -float(K * WSUM), 0.0, ALU.add, ALU.max),
+               [(bk, 0, n)], [("num", col, col + n)], ("c", n), tag="conv%d" % t)
+            step = pl["fargat"] if w == "far" else pl["gat"]
+            for c, k, m in spans:
+                for d in range(0, m, step):
+                    gather(col + c + d, k + d, min(step, m - d))
+            col += n
 
-        def gather(eng, lo, hi):
-            def fn():
-                src = T.lutb[:, 0:W].indirect(T.num16[:, lo:hi])
-                if eng == "V":
-                    return [V.tensor_copy(T.gat[:, 16 * lo:16 * hi], src)]
-                return [A.activation(T.gat[:, 16 * lo:16 * hi], src, ACT.Copy)]
-            op(eng, fn, ["lutb", ("num16", lo, hi)], [("gat", lo, hi)], ("ga", 16 * (hi - lo)), tag="gat%d_%d" % (t, lo))
-
-        def hsum(lo, hi, eng):
-            bk = bank("ph")
+        def front(i, lo, hi):
             n = hi - lo
-            for j0 in range(0, 16, 4):
-                def fn(j0=j0):
-                    out = [P.matmul(T[bk][:, 0:n], T.ident[:], T.gat[:, 16 * lo + j:16 * hi:16], j == 0, j == 15)
-                           for j in range(j0, j0 + 4)]
-                    return out[-1:] if j0 == 12 else []
-                op("P", fn, ["ident", ("gat", lo, hi)], [(bk, 0, n)], ("p", 4 * max(64, n)), tag="h%d_%d" % (t, lo), join=j0 > 0)
-            if eng == "V":
-                op("V", lambda: ts(T.r16[:, lo:hi], T[bk][:, 0:n], 0.0, None, ALU.max), [(bk, 0, n)], [("r16", lo, hi)],
-                   ("c", n), tag="relu%d_%d" % (t, lo))
-            else:
-                op("S", lambda: [A.activation(T.r16[:, lo:hi], T[bk][:, 0:n], ACT.Relu)], [(bk, 0, n)], [("r16", lo, hi)],
-                   ("c", n), tag="relu%d_%d" % (t, lo))
-
-        def tail(lo, hi, et, eq):
-            n = hi - lo
-            pw, pu, pc, po = bank("pw"), bank("pu"), bank("pc"), bank("po")
-            spans = []
-            for s in range(lo, hi):
-                c = column(s)
-                if spans and spans[-1][2] + spans[-1][3] == c:
-                    spans[-1][3] += 1
-                else:
-                    spans.append([s - lo, s, c, 1])
-            for c0, s, c, m in sorted(spans, key=lambda z: z[2]):
-                def fn(c0=c0, s=s, c=c, m=m):
-                    P.matmul(T[pw][:, c0:c0 + m], T.ibig[:], B[:, s:s + m], True, False)
-                    return [P.matmul(T[pw][:, c0:c0 + m], T.pol16[:], T.r16[:, c:c + m], False, True)]
-                op("P", fn, ["ibig", "pol16", (bn, s, s + m), ("r16", c, c + m)], [(pw, c0, c0 + m)],
-                   ("p", max(64, m) * 2), tag="z%d_%d" % (t, s))
+            pa, pb = BANKS[2 * (i % 3)], BANKS[2 * (i % 3) + 1]
+            mm([(T[pb][:, 0:n], T.ibig[:], B[:, lo:hi], n)], ["ibig", (bn, lo, hi)], [(pb, 0, n)], "zb%d" % t,
+               arrived(range(lo // CAP, (hi - 1) // CAP + 1)), stop=False)
+            pc = plan["piece"]
+            for a, b in runs(pl["h"]):
+                for j0 in range(0, 16, pc) if lo <= a < hi else ():
+                    mm([(T[pa][:, a - lo:b - lo], T.ident[:], T.gat[:, 16 * a + j:16 * b:16], b - a) for j in range(j0, j0 + pc)],
+                       ["ident", ("gat", a, b)], [(pa, a - lo, b - lo)], "h%d_%d" % (t, a), start=j0 == 0, stop=j0 + pc == 16)
+            affine(T.relu[:, lo:hi], T[pa][:, 0:n], 1.0, 0.0, [(pa, 0, n)], [("relu", lo, hi)], n, True, "relu%d_%d" % (t, lo))
+            mm([(T[pb][:, 0:n], T.pol16[:], T.relu[:, lo:hi], n)], ["pol16", ("relu", lo, hi)], [(pb, 0, n)], "z%d" % t, start=False)
             half = 0.5 - 0.5 / BIG
-            if et == "V":
-                op("V", lambda: ts(T.tt[:, lo:hi], T[pw][:, 0:n], 1.0 / BIG, half, ALU.mult, ALU.add),
-                   [(pw, 0, n)], [("tt", lo, hi)], ("c", n), tag="t%d_%d" % (t, lo))
-            else:
-                op("S", lambda: [A.activation(T.tt[:, lo:hi], T[pw][:, 0:n], ACT.Identity, half, 1.0 / BIG)],
-                   [(pw, 0, n)], [("tt", lo, hi)], ("c", n), tag="t%d_%d" % (t, lo))
-            op("V", lambda: ts(T.ee[:, lo:hi], T.tt[:, lo:hi], K + 4.0, -4.0, ALU.is_ge, ALU.mult),
-               [("tt", lo, hi)], [("ee", lo, hi)], ("c", n // 2), tag="e%d_%d" % (t, lo))
-
-            def fu():
-                P.matmul(T[pu][:, 0:n], T.bt[:], T.tt[:, lo:hi], True, False)
-                return []
-            op("P", fu, ["bt", ("tt", lo, hi)], [(pu, 0, n)], ("p", max(64, n)), tag="u%d_%d" % (t, lo))
-            op("P", lambda: [P.matmul(T[pu][:, 0:n], T.bt[:], T.ee[:, lo:hi], False, True)], [("ee", lo, hi)], [(pu, 0, n)],
-               ("p", max(64, n)), tag="ue%d_%d" % (t, lo), join=True)
-            if eq == "V":
-                op("V", lambda: ts(T.qq[:, lo:hi], T[pu][:, 0:n], T.init[:, 1:2], 0.0, ALU.add, ALU.max), ["init", (pu, 0, n)],
-                   [("qq", lo, hi)], ("c", n), tag="q%d_%d" % (t, lo))
-            else:
-                op("S", lambda: [A.activation(T.qq[:, lo:hi], T[pu][:, 0:n], ACT.Relu, T.init[:, 1:2], 1.0)], ["init", (pu, 0, n)],
-                   [("qq", lo, hi)], ("c", n), tag="q%d_%d" % (t, lo))
-            op("P", lambda: [P.matmul(T[pc][:, 0:n], T.dd[:], T.qq[:, lo:hi], True, True)], ["dd", ("qq", lo, hi)],
-               [(pc, 0, n)], ("p", max(64, n)), tag="ind%d_%d" % (t, lo))
+            op("V", lambda e: ts(T.tt[:, lo:hi], T[pb][:, 0:n], 1.0 / BIG, half, ALU.mult, ALU.add)
+               + ts(T.ee[:, lo:hi], T[pb][:, 0:n], (K + 3) * BIG + 1, -4.0, ALU.is_ge, ALU.mult),
+               [(pb, 0, n)], [("tt", lo, hi), ("ee", lo, hi)], ("c", 2 * max(n, 64) + 40), tag="te%d_%d" % (t, lo))
+            mm([(T[pa][:, 0:n], T.bt[:], T.tt[:, lo:hi], n), (T[pa][:, 0:n], T.bt[:], T.ee[:, lo:hi], n)],
+               ["bt", ("tt", lo, hi), ("ee", lo, hi)], [(pa, 0, n)], "u%d" % t)
+            affine(T.qq[:, 8 + lo:8 + hi], T[pa][:, 0:n], 1.0, T.init[:, 0:1], ["init", (pa, 0, n)], [("qq", 8 + lo, 8 + hi)], n, True,
+                   "q%d_%d" % (t, lo))
             if last:
-                op("S", lambda: [A.activation(T.t0[:, lo:hi], T.tt[:, lo:hi], ACT.Identity, -float(K), 1.0)],
-                   [("tt", lo, hi)], [("t0", lo, hi)], ("c", n), tag="tz_%d" % lo)
-            first = T.init[:, 0:1] if lo == 0 else T.cum[:, lo - 1:lo]
-            op("V", lambda: [V.tensor_tensor_scan(T.cum[:, lo:hi], T[pc][:, 0:n], T.zero[:, lo:hi], first, ALU.add, ALU.add)],
-               [(pc, 0, n), "zero", "init", ("cum", max(lo - 1, 0), lo)], [("cum", lo, hi)], ("c", n), tag="scan%d_%d" % (t, lo))
-            op("V", lambda: [V.tensor_tensor(T.val[:, lo:hi], T[pc][:, 0:n], T.cum[:, lo:hi], ALU.mult)],
-               [(pc, 0, n), ("cum", lo, hi)], [("val", lo, hi)], ("c", n), tag="val%d_%d" % (t, lo))
-            k = n // 16
+                affine(T.t0[:, lo:hi], T.tt[:, lo:hi], 1.0, -float(K), [("tt", lo, hi)], [("t0", lo, hi)], n, tag="t0_%d" % lo)
 
-            def fw():
-                out = []
-                for i in range(16):
-                    out = [P.matmul(T[po][:, 0:k], T.wd[:, 15 - i:143 - i], T.val[:, lo + i:hi:16], i == 0, i == 15)]
-                return out
-            op("P", fw, ["wd", ("val", lo, hi)], [(po, 0, k)], ("p", 16 * 64), tag="wrap%d_%d" % (t, lo))
-            op("V", lambda: ts(T.pos16[:, lo // 16:hi // 16], T[po][:, 0:k], float(MID), None, ALU.add),
-               [(po, 0, k)], [("pos16", lo, hi)], ("c", k), tag="pos%d_%d" % (t, lo))
+        def back(i, lo, hi, p):
+            n, k, a, b = hi - lo, (hi - lo) // 16, lo // 2, hi // 2
+            m = b - a
+            pa, pb = BANKS[2 * (i % 3)], BANKS[2 * (i % 3) + 1]
+            mm([(T[pb][:, 0:m], w, T.qq[:, 8 + lo + d:8 + hi + d:2], m) for w, d in earlier],
+               ["both", "ddx", ("qq", 7 + lo, 8 + hi)], [(pb, 0, m)], "cnt%d" % t)
+            mm([(T[pa][:, 0:m], same[d], T.qq[:, 8 + lo + d:8 + hi:2], m) for d in range(2)], ["ddx", ("qq", 8 + lo, 8 + hi)],
+               [(pa, 0, m)], "ind%d" % t)
+            first = T.init[:, 2:3] if lo == 0 else T.cum[:, a - 1:a]
+            op("V", lambda e: [V.tensor_tensor_scan(T.cum[:, a:b], T[pb][:, 0:m], T.step[:, a:b], first, ALU.add, ALU.add)],
+               [(pb, 0, m), "step", "init", ("cum", max(a - 1, 0), a)], [("cum", a, b)], ("c", m), tag="scan%d_%d" % (t, lo))
+            op("V", lambda e: [V.tensor_tensor(T.val[:, a:b], T[pa][:, 0:m], T.cum[:, a:b], ALU.mult)],
+               [(pa, 0, m), ("cum", a, b)], [("val", a, b)], ("c", m), tag="val%d_%d" % (t, lo))
+            mm([(T[pb][:, 0:k], T.ones[0:1, :], T.mrow[0:1, lo // 16:hi // 16], k)], ["ones", "mrow"], [(pb, 0, k)],
+               "spare%d" % t, stop=False)
+            mm([(T[pb][:, 0:k], T.wd[:, 14 - 2 * j:142 - 2 * j], T.val[:, a + j:b:8], k) for j in range(8)], ["wd", ("val", a, b)],
+               [(pb, 0, k)], "wrap%d" % t, start=False)
+            op("V", lambda e: ts(T.pos[:, p:p + k], T[pb][:, 0:k], T.init[:, 1:2], None, ALU.add),
+               [(pb, 0, k), "init"], [("pos", p, p + k)], ("c", k), tag="pos%d_%d" % (t, lo))
             tb = "t0" if last else "tt"
-            op("V", lambda: [V.tensor_tensor(Wn[:, 0:WIN].indirect(T.pos16[:, lo // 16:hi // 16]), T[tb][:, lo:hi],
-                                             T.ee[:, lo:hi], ALU.add)],
-               [("pos16", lo, hi), (tb, lo, hi), ("ee", lo, hi)], [wn], ("sc", n), tag="scat%d_%d" % (t, lo))
+            op("V", lambda e: [V.tensor_tensor(Wn[:, 0:WIN].indirect(T.pos[:, p:p + k]), T[tb][:, lo:hi], T.ee[:, lo:hi], ALU.add)],
+               [("pos", p, p + k), (tb, lo, hi), ("ee", lo, hi)], [wn], ("sc", n), tag="scat%d_%d" % (t, lo))
 
-        for lo, hi in runs(pl["conv"]):
-            conv(lo, hi)
-        for (e, n), (lo, hi) in zip(pl["gat"], runs([n for e, n in pl["gat"]])):
-            gather(e, lo, hi)
-        tails = [z + (a, b) for (n, a, b), z in zip(pl["tail"], runs([n for n, a, b in pl["tail"]]))]
-        for (n, e), (lo, hi) in zip(pl["h"], runs([n for n, e in pl["h"]])):
-            hsum(lo, hi, e)
-            while tails and all(column(s) < hi for s in range(tails[0][0], tails[0][1])):
-                tail(*tails.pop(0))
+        backs = runs(pl["back"])
+        p = 0
+        for i, (lo, hi) in enumerate(runs(pl["front"])):
+            front(i, lo, hi)
+            while backs and backs[0][1] <= hi:
+                a, b = backs.pop(0)
+                back(i, a, b, p)
+                p += ((b - a) // 16 + 1) // 2 * 2
 
-        dm, om, _ = masks(T, topo, me, t)
-
-        def send():
+        def send(e):
             tr = []
-            for (h, r), (m, n) in zip(hands, om):
-                rid, pid = topo.addr(h, core)
+            for (c, r), (m, n) in zip(hands, om):
+                rid, pid = topo.addr(c, core)
                 tr.append(RemoteDMATransfer(dst_ids=[DstId(rid=rid, pnc=pid)], dma_engine_mask=m, remote_sem=T.sem["hop%d" % t],
-                                            src=Wn[:, r * STRIDE:r * STRIDE + CAP], dst=T["hand%d" % t][:]))
-            if t in HELPERS_FIRST:
-                g.remote_dma_fused(tr, local_sem=T.sem.left)
-                tr = []
+                                            src=Wn[:, part(r):part(r) + CAP], dst=T["hand%d" % t][:]))
+            g.remote_dma_fused(tr, local_sem=T.sem.left)
+            tr = []
             for k, (r, (m, n)) in enumerate(zip(direct, dm)):
                 rid, pid = topo.addr(T.cores[r], core)
                 tr.append(RemoteDMATransfer(dst_ids=[DstId(rid=rid, pnc=pid)], dma_engine_mask=m,
                                             remote_sem=T.sem[("dir%d" if k else "soon%d") % t],
-                                            src=Wn[:, r * STRIDE:r * STRIDE + CAP], dst=T[nb][:, me * CAP:(me + 1) * CAP]))
+                                            src=Wn[:, part(r):part(r) + CAP], dst=T[nb][:, me * CAP:(me + 1) * CAP]))
             g.remote_dma_fused(tr, local_sem=T.sem.left)
             return []
-        op("G", send, [wn], [], ("c", 500), tag="send%d" % t)
-        p = me * STRIDE
-        op("S", lambda: [A.activation(T[nb][:, me * CAP:(me + 1) * CAP], Wn[:, p:p + CAP], ACT.Copy)],
-           [(wn, p, p + CAP)], [(nb, me * CAP, (me + 1) * CAP)], ("c", 48), tag="own%d" % t)
-        return sum(n for m, n in dm + om)
+        sent = op("G", send, [wn], [], ("c", 500), tag="send%d" % t)
+        ops[-1]["sends"] = t
+        p = part(me)
+        affine(T[nb][:, me * CAP:(me + 1) * CAP], Wn[:, p:p + CAP], 1.0, 0.0, [(wn, p, p + CAP)], [(nb, me * CAP, (me + 1) * CAP)],
+               CAP, tag="own%d" % t)
+        if not last:
+            clear(t + 1, sent)
 
-    left = sum([ply(t) for t in range(RO)])
-    op("Y", lambda: [g.sync.dma_start(T.y[:], T["brd%d" % RO][:])], ["brd%d" % RO], [], ("d", "small"),
+    for t in range(RO):
+        ply(t)
+    op("Y", lambda e: [g.sync.dma_start(T.y[:], T["brd%d" % RO][:])], ["brd%d" % RO], [], ("d", "small"),
        [("%s%d" % (w, RO - 1), way[w][0], w, RO - 1) for w in way], "store", own="sty")
-    return ops, left
+    return ops, RO * sum(n for m, n in dm + om)
 
 
 def depend(ops):
@@ -360,14 +337,13 @@ def depend(ops):
         for a, isw in acc:
             for j, (b, lo, hi), jw in seen.get(a[0], []):
                 meet = lo < a[2] and a[1] < hi and (isw or jw)
-                if ops[j]["eng"] != o["eng"]:
-                    if meet or b in BANKS:
+                if b in BANKS and o["eng"] == "P" == ops[j]["eng"]:
+                    if meet and not o["join"]:
                         dep[j] = True
-                elif meet and not o["join"]:
-                    dep[j] = True
-                elif b in BANKS and o["eng"] == "P":
                     dep.setdefault(j, False)
-        if "behind" in o:
+                elif meet or b in BANKS:
+                    dep[j] = True
+        if o["behind"] is not None:
             dep.setdefault(o["behind"], False)
         o["dep"] = dep
         for a, isw in acc:
@@ -382,15 +358,15 @@ def span(o, c):
     if kind == "p":
         d = 12 + n * c["pe"] * c["f"]
     elif kind == "c":
-        d = 40 + max(64, n) * cyc
+        d = 30 + max(64, n) * cyc
     else:
         d = {"g": 170 + 2 * n * cyc, "ga": 60 + n * c["gam"] * cyc, "sc": 60 + n * c["sig"] * cyc}[kind]
     return d, d
 
 
-def arrange(ops, c, look, fixed=None):
+def arrange(ops, c, look):
     n = len(ops)
-    sent = {int(o["tag"][4:]): i for i, o in enumerate(ops) if o["tag"].startswith("send")}
+    sent = {o["sends"]: i for i, o in enumerate(ops) if "sends" in o}
     sp = [span(o, c) for o in ops]
     pre = [set(o["dep"]) | set(sent[e[3]] for e in o["ext"]) for o in ops]
     post = [[] for o in ops]
@@ -399,34 +375,38 @@ def arrange(ops, c, look, fixed=None):
             post[j].append(i)
     rank = [0.0] * n
     for i in range(n - 1, -1, -1):
-        rank[i] += sp[i][1] + ops[i]["bias"]
-        for j in ops[i]["dep"]:
-            rank[j] = max(rank[j], rank[i] + c["sem"])
+        rank[i] += sp[i][1]
+        for j, wt in ops[i]["dep"].items():
+            rank[j] = max(rank[j], rank[i] + c["sem"] if wt else rank[i] - sp[j][1] + sp[j][0])
         for e in ops[i]["ext"]:
             rank[sent[e[3]]] = max(rank[sent[e[3]]], rank[i] + c[e[2]])
-    end, start, out = [None] * n, [None] * n, []
-    free = {e: 0.0 for e in "VSPGY"}
+    end, start = [None] * n, [None] * n
+    busy = {e: [] for e in "SVPGY"}
     missing = [len(p) for p in pre]
     ready = {i: 0.0 for i in range(n) if not pre[i]}
-    heads = None if fixed is None else {e: [i for i in fixed if ops[i]["eng"] == e] for e in free}
+
+    def gap(e, s, d):
+        for a, b in busy[e]:
+            if s + d <= a:
+                break
+            s = max(s, b)
+        return s
     while ready:
-        pool = ready if heads is None else [q[0] for q in heads.values() if q and q[0] in ready]
-        cand = [(max(ready[i], free[ops[i]["eng"]]), i) for i in pool]
-        s0, i0 = min(cand)
-        s, i = max([z for z in cand if ops[z[1]]["eng"] == ops[i0]["eng"] and z[0] <= s0 + look], key=lambda z: rank[z[1]])
+        i = max(ready, key=lambda z: rank[z] - (c["yield"] if ops[z]["cost"][0] == "ga" else 0.0))
+        o = ops[i]
+        s, e = min((gap(e, ready[i], sp[i][0]), e) for e in ("SV" if o["eng"] == "F" else o["eng"]))
+        if o["eng"] == "F" and gap("S", ready[i], sp[i][0]) <= s + look:
+            s, e = gap("S", ready[i], sp[i][0]), "S"
+        o["eng"] = e
         start[i], end[i] = s, s + sp[i][1]
-        free[ops[i]["eng"]] = s + sp[i][0]
-        out.append(i)
+        busy[e] = sorted(busy[e] + [(s, s + sp[i][0])])
         del ready[i]
-        if heads is not None:
-            heads[ops[i]["eng"]].pop(0)
         for k in post[i]:
             missing[k] -= 1
             if not missing[k]:
-                o = ops[k]
-                ready[k] = max([end[j] + c["sem"] if wt else start[j] for j, wt in o["dep"].items()]
-                               + [start[sent[e[3]]] + c[e[2]] for e in o["ext"]])
-    return out, start, end
+                ready[k] = max([end[j] + c["sem"] if wt else start[j] + sp[j][0] for j, wt in ops[k]["dep"].items()]
+                               + [start[sent[e[3]]] + c[e[2]] + (c["first"] if e[3] == 0 else 0.0) for e in ops[k]["ext"]])
+    return sorted(range(n), key=lambda z: (start[z], z)), start, end
 
 
 def emit(g, T, ops, order, left):
@@ -452,7 +432,7 @@ def emit(g, T, ops, order, left):
                 know[e][s] = v
                 for s2, v2 in after.get((s, v), {}).items():
                     know[e][s2] = max(know[e].get(s2, 0), v2)
-        ins = o["fn"]()
+        ins = o["fn"](e)
         if o["own"]:
             ins[0].then_inc(T.sem[o["own"]], 16)
             mark[i] = (o["own"], 16)
@@ -473,18 +453,16 @@ def emit(g, T, ops, order, left):
 
 def helper_program(g, core, T, topo):
     for a in range(N):
-        for i, (h, r) in enumerate(routes(T, topo, a)[1]):
-            if h != core:
+        for i, (c, r) in enumerate(routes(T, topo, a)[1]):
+            if c != core:
                 continue
             rid, pid = topo.addr(T.cores[r], core)
-            total = 0
+            _, om, hm = masks(T, topo, a)
             for t in range(RO):
-                _, om, hm = masks(T, topo, a, t)
                 g.wait_ge(T.sem["hop%d" % t], om[i][1])
                 g.remote_dma(T["brd%d" % (t + 1)][:, a * CAP:(a + 1) * CAP], T["hand%d" % t][:], T.sem["far%d" % t], T.sem.left,
                              pid, rid, hm[i][0])
-                total += hm[i][1]
-            g.wait_ge(T.sem.left, total)
+            g.wait_ge(T.sem.left, RO * hm[i][1])
 
 
 def rank_program(g, core, T, topo):

@@ -15,10 +15,10 @@ SCRATCH = {"pol16": ("sbuf", [128, 128], "float16"), "wd": ("sbuf", [128, 144], 
            "rows": ("sbuf", [128, 392], "float32"), "mrow": ("sbuf", [128, 32], "bfloat16"), "wd0": ("sbuf", [128, 144], "bfloat16"),
            "lutb": ("sbuf", [128, W], "bfloat16"), "gat": ("sbuf", [128, 16 * S], "bfloat16"), "qq": ("sbuf", [128, S + 16], "bfloat16"),
            "pos": ("sbuf", [128, 48], "uint16")}
-for _n in ("plb", "polb", "ones", "ident", "ibig", "bt", "both"):
+for _n in ("plb", "pl2", "polb", "ones", "ident", "ibig", "ibig2", "bt", "both"):
     SCRATCH[_n] = ("sbuf", [128, 128], "bfloat16")
 for _n, _d in (("num", "uint16"), ("relu", "float16"), ("tt", "bfloat16"), ("ee", "bfloat16"), ("t0", "bfloat16"), ("cum", "float32"),
-               ("val", "float16"), ("xb", "bfloat16"), ("xm", "bfloat16")):
+               ("val", "float16"), ("xm", "bfloat16"), ("e0", "bfloat16")):
     SCRATCH[_n] = ("sbuf", [128, S], _d)
 for _t in range(RO + 1):
     SCRATCH["brd%d" % _t] = ("sbuf", [128, S], "bfloat16")
@@ -26,18 +26,26 @@ for _t in range(RO):
     SCRATCH["win%d" % _t] = ("sbuf", [128, WIN], "bfloat16")
     SCRATCH["hand%d" % _t] = ("sbuf", [128, CAP], "bfloat16")
 BANKS = tuple("bank%d" % _b for _b in range(8))
+PAIRS = (BANKS[0:2], BANKS[2:4], BANKS[6:8])
 for _n in BANKS:
     SCRATCH[_n] = ("psum", [128, 512], "float32")
 
 SEMAPHORES = ["cv", "cs", "cp", "cg", "ldx", "ldpl", "ldpol", "ldlut", "sty", "left"]
+WAYS = ("da", "db", "dc", "dd", "far")
 for _t in range(RO):
-    SEMAPHORES += ["%s%d" % (_w, _t) for _w in ("soon", "dir", "far", "hop")]
+    SEMAPHORES += ["%s%d" % (_w, _t) for _w in WAYS + ("hop",)]
 
-PLAN = {"first": {"gat": 24, "conv": [4, 4], "h": [96, 96, 96, 48, 48], "front": [192, 96, 96], "back": [192, 96, 96]},
-        "later": {"gat": 24, "fargat": 24, "conv": [2, 2, 2], "h": [1, 3, 5], "front": [3, 5], "back": [3]},
-        "look": 0.0, "piece": 2}
-COST = {"f": 1.0, "gam": 1.56, "sig": 3.0, "pe": 0.42, "sem": 220.0, "load": 4200.0, "pol": 4600.0, "first": 1500.0,
-        "small": 1600.0, "soon": 1800.0, "dir": 3000.0, "far": 3000.0, "yield": 0.0}
+PLAN = {"first": {"gat": [72, 72, 72, 72, 56, 40], "conv": [4, 4], "h": [144, 144, 96], "front": [144, 144, 96],
+                  "back": [144, 144, 96], "scat": [144, 144, 96], "bias": {}},
+        "later": {"gat": [24] * 4 + [48] * 4 + [32, 32, 16, 16], "conv": [2, 2, 2], "h": [96, 96, 96, 48, 48], "front": [3, 1],
+                  "back": [3], "scat": [3], "bias": {"relu2": 400.0}},
+        "second": {"gat": [24] * 4 + [48, 48, 40, 56, 40, 56], "conv": [2, 2], "h": [48, 144, 96, 96], "front": [3, 2],
+                   "back": [2], "scat": [2], "bias": {}},
+        "early": [[[0], [1, 2]], [[0]], []],
+        "calls": [[[3, 4, 5, 6], [0], [1, 2]]] * RO, "helpers": [2, 3, 0, 1],
+        "cast": "F", "look": 0.0, "piece": 4}
+COST = {"f": 1.05, "gam": 1.56, "sig": 3.0, "pe": 0.3, "mm": 60, "sem": 200.0, "load": 3400.0, "pol": 4600.0, "small": 1600.0,
+        "come": [{"da": 2300.0, "db": 3400.0, "far": 4600.0}, {"da": 1500.0, "far": 3000.0}, {"far": 3000.0}]}
 
 
 def routes(T, topo, a):
@@ -46,7 +54,8 @@ def routes(T, topo, a):
     direct = [r for r in ring if topo.may_write(src, T.cores[r])]
     far = [r for r in ring if r not in direct]
     helpers = [c for c in topo.cores_of(src) if T.rank_of(c) is None and all(topo.may_write(c, T.cores[r]) for r in far)]
-    return direct, list(zip(helpers, far))
+    helpers.sort(key=lambda c: topo.die(c) != topo.die(src))
+    return direct, list(zip([helpers[k] for k in PLAN["helpers"]], far))
 
 
 def shares(engines, n):
@@ -60,29 +69,33 @@ def shares(engines, n):
     return out
 
 
-def masks(T, topo, a):
+def masks(T, topo, a, t):
     src = T.cores[a]
     direct, hands = routes(T, topo, a)
     off = topo.engines(src, T.cores[direct[0]])
     on = topo.engines(src, hands[0][0])
-    hm = [shares(topo.engines(h, T.cores[r]), 1)[0] for h, r in hands]
-    return shares(off, len(direct)), shares(on, len(hands)), hm
+    out = {}
+    for call in PLAN["calls"][t]:
+        away, here = [k for k in call if k < len(direct)], [k for k in call if k >= len(direct)]
+        out.update(zip(away, shares(off, len(away)) if away else []))
+        out.update(zip(here, shares([e for e in on if not away or e not in off], len(here)) if here else []))
+    return [out[k] for k in range(N - 1)], [shares(topo.engines(h, T.cores[r]), 1)[0] for h, r in hands]
 
 
-def arrivals(T, topo, me):
-    way = {"soon": [0, []], "dir": [0, []], "far": [0, []]}
+def way_of(t, k):
+    return ([w for w, z in zip(WAYS, PLAN["early"][t]) if k in z] + [WAYS[-1]])[0]
+
+
+def arrivals(T, topo, me, t):
+    way = {w: [0, []] for w in WAYS[:len(PLAN["early"][t])] + WAYS[-1:]}
     for a in range(N):
         if a == me:
             continue
         direct, hands = routes(T, topo, a)
-        dm, _, hm = masks(T, topo, a)
-        if me in direct:
-            k = direct.index(me)
-            w, n = ("soon" if k == 0 else "dir"), dm[k][1]
-        else:
-            w, n = "far", hm[[r for h, r in hands].index(me)][1]
-        way[w][0] += n
-        way[w][1].append(a)
+        first, second = masks(T, topo, a, t)
+        k = (direct + [r for h, r in hands]).index(me)
+        way[way_of(t, k)][0] += (first[:len(direct)] + second)[k][1]
+        way[way_of(t, k)][1].append(a)
     return way
 
 
@@ -100,11 +113,13 @@ def part(r):
 
 def make_ops(g, core, T, topo, me, plan):
     ops = []
+    now = {"bias": {}, "run": ""}
     V, A, P = g.vector, g.scalar, g.tensor
 
     def op(eng, fn, reads=(), writes=(), cost=("c", 64), ext=(), tag="", join=False, own=None, behind=None):
         ops.append({"eng": eng, "fn": fn, "r": [whole(a) for a in reads], "w": [whole(a) for a in writes], "cost": cost,
-                    "ext": list(ext), "tag": tag, "join": join, "own": own, "behind": behind})
+                    "ext": list(ext), "tag": tag, "join": join, "own": own, "behind": behind,
+                    "bias": now["bias"].get(tag.rstrip("0123456789_") + now["run"], 0.0)})
         return len(ops) - 1
 
     def whole(a):
@@ -139,12 +154,12 @@ def make_ops(g, core, T, topo, me, plan):
         def fn(e):
             out = [P.matmul(o, l, r, start and i == 0, stop and i == len(steps) - 1) for i, (o, l, r, n) in enumerate(steps)]
             return out[-1:] if stop else []
-        op("P", fn, reads, writes, ("p", sum(max(64, z[3]) for z in steps)), ext, tag, join=not start)
+        op("P", fn, reads, writes, ("p", sum(COST["mm"] + max(64, z[3]) for z in steps)), ext, tag, join=not start)
 
     def load(queue, name, src, cost, sem, behind=None):
         q = {"S": A, "Y": g.sync}[queue]
         return op(queue, lambda e: [q.dma_start(T[name][:], src[:])], [], [name], ("d", cost), own=sem, behind=behind)
-    load("S", "xb", T.x, "small", "ldx")
+    load("S", "brd0", T.x, "small", "ldx")
     i = load("Y", "plb", T.pl, "small", "ldpl")
     i = load("Y", "lutb", T.lut, "load", "ldlut", i)
     load("Y", "polb", T.pol, "pol", "ldpol", i)
@@ -152,8 +167,10 @@ def make_ops(g, core, T, topo, me, plan):
     fill("ident", 1.0)
     select("ident", [[-1, 128]], ALU.is_equal, 0, 1)
     affine(T.ibig[:], T.ident[:], BIG, 0.0, ["ident"], ["ibig"], 128)
+    affine(T.ibig2[:], T.ident[:], 2 * BIG, 0.0, ["ident"], ["ibig2"], 128)
+    affine(T.pl2[:], T.plb[:], 2.0, 0.0, ["plb"], ["pl2"], 128)
     affine(T.pol16[:], T.polb[:], 1.0, 0.0, ["polb"], ["pol16"], 128)
-    fill("bt", 0.125)
+    fill("bt", 0.25)
     select("bt", [[0, 8], [-1, 16]], ALU.is_ge, N, 0)
     select("bt", [[-16, 8], [0, 16]], ALU.is_ge, 0, 1)
     select("bt", [[16, 8], [0, 16]], ALU.is_ge, 15, -1)
@@ -183,8 +200,7 @@ def make_ops(g, core, T, topo, me, plan):
     affine(T.wd[:], T.wd0[:], 1.0, 0.0, ["wd0"], ["wd"], 144)
     fill("qq", 0.0, slice(0, 8))
 
-    op("V", lambda e: ts(T.xm[:], T.xb[:], 0.0, float(K), ALU.is_ge, ALU.mult), ["xb"], ["xm"], ("c", S // 2))
-    op("V", lambda e: [V.tensor_tensor(T.brd0[:], T.xm[:], T.xb[:], ALU.add)], ["xm", "xb"], ["brd0"], ("c", 2 * S))
+    op("V", lambda e: ts(T.xm[:], T.brd0[:], 0.0, float(K), ALU.is_ge, ALU.mult), ["brd0"], ["xm"], ("c", S // 2))
 
     def clear(t, behind):
         wn = "win%d" % t
@@ -193,31 +209,54 @@ def make_ops(g, core, T, topo, me, plan):
     clear(0, None)
 
     direct, hands = routes(T, topo, me)
-    way = arrivals(T, topo, me)
-    dm, om, _ = masks(T, topo, me)
+    left = [0]
 
     def ply(t):
-        pl = plan["first"] if t == 0 else plan["later"]
-        last = t == RO - 1
+        way = arrivals(T, topo, me, t - 1)
+        sm = masks(T, topo, me, t)[0]
+        left[0] += sum(n for m, n in sm)
+        pl = plan["first"] if t == 0 else dict(plan["later"], **(plan["second"] if t == 1 else {}))
+        last, kt = t == RO - 1, K + 2 * t
+        pw, big = ("pl2", "ibig2") if t else ("plb", "ibig")
+        now.update(bias=pl["bias"], run="")
         bn, wn, nb = "brd%d" % t, "win%d" % t, "brd%d" % (t + 1)
         B, Wn = T[bn], T[wn]
         if t == 0:
             lots = [(None, list(range(a, b))) for a, b in runs(pl["conv"])]
         else:
-            late = sorted(way["far"][1] + way["dir"][1])
-            lots = [(None, [me]), ("soon", way["soon"][1])] + [("far", late[a:b]) for a, b in runs(pl["conv"])]
+            late = sorted(way["far"][1])
+            lots = ([(None, [me])] + [(w, sorted(way[w][1])) for w in way if w != "far"]
+                    + [("far", late[a:b]) for a, b in runs(pl["conv"]) if late[a:b]])
             pl = dict(pl)
-            for z in ("h", "front", "back"):
-                cut = [0] + [CAP * late[k] for k in pl[z]] + [S]
-                pl[z] = [b - a for a, b in zip(cut, cut[1:]) if b > a]
+            for z in ("front", "back", "scat"):
+                cut = [0] + [CAP * late[-k] for k in pl[z]] + [S]
+                pl[z] = [b - a for a, b in zip(cut, cut[1:])]
+        order = [a for w, blocks in lots for a in blocks]
 
-        def gather(c, k, n):
+        def pieces(lo, hi):
+            out = []
+            for s in range(lo, hi):
+                c = order.index(s // CAP) * CAP + s % CAP
+                if out and out[-1][1] + out[-1][2] == c:
+                    out[-1][2] += 1
+                else:
+                    out.append([s, c, 1])
+            return sorted(out, key=lambda z: z[1])
+
+        def gather(c, n):
             def fn(e):
                 src = T.lutb[:, 0:W].indirect(T.num[:, c:c + n])
                 if e == "V":
-                    return [V.tensor_copy(T.gat[:, 16 * k:16 * (k + n)], src)]
-                return [A.activation(T.gat[:, 16 * k:16 * (k + n)], src, ACT.Copy)]
-            op("F", fn, ["lutb", ("num", c, c + n)], [("gat", k, k + n)], ("ga", 16 * n), tag="gat%d_%d" % (t, k))
+                    return [V.tensor_copy(T.gat[:, 16 * c:16 * (c + n)], src)]
+                return [A.activation(T.gat[:, 16 * c:16 * (c + n)], src, ACT.Copy)]
+            op("F", fn, ["lutb", ("num", c, c + n)], [("gat", c, c + n)], ("ga", 16 * n), tag="gat%d_%d" % (t, c))
+
+        def hsum(i, a, b):
+            bk, pc = BANKS[4 + i % 2], plan["piece"]
+            for j0 in range(0, 16, pc):
+                mm([(T[bk][:, 0:b - a], T.ident[:], T.gat[:, 16 * a + j:16 * b:16], b - a) for j in range(j0, j0 + pc)],
+                   ["ident", ("gat", a, b)], [(bk, 0, b - a)], "h%d_%d" % (t, a), start=j0 == 0, stop=j0 + pc == 16)
+            affine(T.relu[:, a:b], T[bk][:, 0:b - a], 1.0, 0.0, [(bk, 0, b - a)], [("relu", a, b)], b - a, True, "relu%d_%d" % (t, a))
 
         def arrived(blocks):
             return [("%s%d" % (w, t - 1), way[w][0], w, t - 1) for w in way if t > 0 and any(a in way[w][1] for a in blocks)]
@@ -232,45 +271,51 @@ def make_ops(g, core, T, topo, me, plan):
                 else:
                     spans.append([j * CAP, a * CAP, CAP])
             n = CAP * len(blocks)
-            op("P", lambda e, bk=bk, spans=spans: [P.matmul(T[bk][:, c:c + m], T.plb[:], B[:, k:k + m], True, True)
+            op("P", lambda e, bk=bk, spans=spans: [P.matmul(T[bk][:, c:c + m], T[pw][:], B[:, k:k + m], True, True)
                                                    for c, k, m in spans][-1:],
-               ["plb"] + [(bn, k, k + m) for c, k, m in spans], [(bk, 0, n)], ("p", sum(max(64, m) for c, k, m in spans)),
+               [pw] + [(bn, k, k + m) for c, k, m in spans], [(bk, 0, n)], ("p", sum(COST["mm"] + max(64, m) for c, k, m in spans)),
                arrived(blocks), "num%d" % t)
-            op("V", lambda e, bk=bk, col=col, n=n: ts(T.num[:, col:col + n], T[bk][:, 0:n], -float(K * WSUM), 0.0, ALU.add, ALU.max),
-               [(bk, 0, n)], [("num", col, col + n)], ("c", n), tag="conv%d" % t)
-            step = pl["fargat"] if w == "far" else pl["gat"]
-            for c, k, m in spans:
-                for d in range(0, m, step):
-                    gather(col + c + d, k + d, min(step, m - d))
+            affine(T.num[:, col:col + n], T[bk][:, 0:n], 1.0, -float(kt * WSUM) if t else 0.0, [(bk, 0, n)], [("num", col, col + n)],
+                   n, True, "conv%d" % t, plan["cast"])
             col += n
+        for (a, b), eng in zip(runs(pl["gat"]), pl.get("by", "F" * S)):
+            gather(a, b - a)
+            ops[-1]["eng"] = eng
+        for i, (a, b) in enumerate(runs(pl["h"])):
+            now["run"] = str(i)
+            hsum(i, a, b)
 
         def front(i, lo, hi):
             n = hi - lo
-            pa, pb = BANKS[2 * (i % 3)], BANKS[2 * (i % 3) + 1]
-            mm([(T[pb][:, 0:n], T.ibig[:], B[:, lo:hi], n)], ["ibig", (bn, lo, hi)], [(pb, 0, n)], "zb%d" % t,
-               arrived(range(lo // CAP, (hi - 1) // CAP + 1)), stop=False)
-            pc = plan["piece"]
-            for a, b in runs(pl["h"]):
-                for j0 in range(0, 16, pc) if lo <= a < hi else ():
-                    mm([(T[pa][:, a - lo:b - lo], T.ident[:], T.gat[:, 16 * a + j:16 * b:16], b - a) for j in range(j0, j0 + pc)],
-                       ["ident", ("gat", a, b)], [(pa, a - lo, b - lo)], "h%d_%d" % (t, a), start=j0 == 0, stop=j0 + pc == 16)
-            affine(T.relu[:, lo:hi], T[pa][:, 0:n], 1.0, 0.0, [(pa, 0, n)], [("relu", lo, hi)], n, True, "relu%d_%d" % (t, lo))
-            mm([(T[pb][:, 0:n], T.pol16[:], T.relu[:, lo:hi], n)], ["pol16", ("relu", lo, hi)], [(pb, 0, n)], "z%d" % t, start=False)
-            half = 0.5 - 0.5 / BIG
-            op("V", lambda e: ts(T.tt[:, lo:hi], T[pb][:, 0:n], 1.0 / BIG, half, ALU.mult, ALU.add)
-               + ts(T.ee[:, lo:hi], T[pb][:, 0:n], (K + 3) * BIG + 1, -4.0, ALU.is_ge, ALU.mult),
-               [(pb, 0, n)], [("tt", lo, hi), ("ee", lo, hi)], ("c", 2 * max(n, 64) + 40), tag="te%d_%d" % (t, lo))
+            pa, pb = PAIRS[i]
+            terms = [bn] if t else [bn, "xm"]
+            mm([(T[pb][:, 0:n], T[big][:], T[z][:, lo:hi], n) for z in terms], [big] + [(z, lo, hi) for z in terms],
+               [(pb, 0, n)], "zb%d" % t, arrived(range(lo // CAP, (hi - 1) // CAP + 1)), stop=False)
+            todo = pieces(lo, hi)
+            for s, c, m in todo:
+                mm([(T[pb][:, s - lo:s - lo + m], T.pol16[:], T.relu[:, c:c + m], m)], ["pol16", ("relu", c, c + m)],
+                   [(pb, s - lo, s - lo + m)], "z%d" % t, start=False, stop=s == todo[-1][0])
+            half, wrap = 0.25 - 0.25 / BIG, (kt + 3) * BIG + 0.5
+
+            def grow(e):
+                if e == "S":
+                    return [A.activation(T.tt[:, lo:hi], T[pb][:, 0:n], ACT.Identity, half, 0.5 / BIG),
+                            A.activation(T.ee[:, lo:hi], T[pb][:, 0:n], ACT.Sign, wrap, -1.0)]
+                return (ts(T.tt[:, lo:hi], T[pb][:, 0:n], 0.5 / BIG, half + 1, ALU.mult, ALU.add)
+                        + ts(T.ee[:, lo:hi], T[pb][:, 0:n], wrap, -2.0, ALU.is_ge, ALU.mult))
+            op("F", grow, [(pb, 0, n)], [("tt", lo, hi), ("ee", lo, hi)], ("c", 2 * max(n, 64) + 40), tag="te%d_%d" % (t, lo))
             mm([(T[pa][:, 0:n], T.bt[:], T.tt[:, lo:hi], n), (T[pa][:, 0:n], T.bt[:], T.ee[:, lo:hi], n)],
                ["bt", ("tt", lo, hi), ("ee", lo, hi)], [(pa, 0, n)], "u%d" % t)
             affine(T.qq[:, 8 + lo:8 + hi], T[pa][:, 0:n], 1.0, T.init[:, 0:1], ["init", (pa, 0, n)], [("qq", 8 + lo, 8 + hi)], n, True,
                    "q%d_%d" % (t, lo))
             if last:
-                affine(T.t0[:, lo:hi], T.tt[:, lo:hi], 1.0, -float(K), [("tt", lo, hi)], [("t0", lo, hi)], n, tag="t0_%d" % lo)
+                affine(T.t0[:, lo:hi], T.tt[:, lo:hi], 2.0, -kt - 2.0, [("tt", lo, hi)], [("t0", lo, hi)], n, tag="t0_%d" % lo)
+                affine(T.e0[:, lo:hi], T.ee[:, lo:hi], 2.0, 0.0, [("ee", lo, hi)], [("e0", lo, hi)], n, tag="e0_%d" % lo)
 
         def back(i, lo, hi, p):
             n, k, a, b = hi - lo, (hi - lo) // 16, lo // 2, hi // 2
             m = b - a
-            pa, pb = BANKS[2 * (i % 3)], BANKS[2 * (i % 3) + 1]
+            pa, pb = PAIRS[i]
             mm([(T[pb][:, 0:m], w, T.qq[:, 8 + lo + d:8 + hi + d:2], m) for w, d in earlier],
                ["both", "ddx", ("qq", 7 + lo, 8 + hi)], [(pb, 0, m)], "cnt%d" % t)
             mm([(T[pa][:, 0:m], same[d], T.qq[:, 8 + lo + d:8 + hi:2], m) for d in range(2)], ["ddx", ("qq", 8 + lo, 8 + hi)],
@@ -284,35 +329,37 @@ def make_ops(g, core, T, topo, me, plan):
                "spare%d" % t, stop=False)
             mm([(T[pb][:, 0:k], T.wd[:, 14 - 2 * j:142 - 2 * j], T.val[:, a + j:b:8], k) for j in range(8)], ["wd", ("val", a, b)],
                [(pb, 0, k)], "wrap%d" % t, start=False)
-            op("V", lambda e: ts(T.pos[:, p:p + k], T[pb][:, 0:k], T.init[:, 1:2], None, ALU.add),
-               [(pb, 0, k), "init"], [("pos", p, p + k)], ("c", k), tag="pos%d_%d" % (t, lo))
-            tb = "t0" if last else "tt"
-            op("V", lambda e: [V.tensor_tensor(Wn[:, 0:WIN].indirect(T.pos[:, p:p + k]), T[tb][:, lo:hi], T.ee[:, lo:hi], ALU.add)],
-               [("pos", p, p + k), (tb, lo, hi), ("ee", lo, hi)], [wn], ("sc", n), tag="scat%d_%d" % (t, lo))
+            affine(T.pos[:, p:p + k], T[pb][:, 0:k], 1.0, T.init[:, 1:2], [(pb, 0, k), "init"], [("pos", p, p + k)], k, True,
+                   "pos%d_%d" % (t, lo), plan["cast"])
 
-        backs = runs(pl["back"])
+        def scatter(lo, hi, p):
+            (tb, eb), k = ("t0", "e0") if last else ("tt", "ee"), (hi - lo) // 16
+            op("V", lambda e: [V.tensor_tensor(Wn[:, 0:WIN].indirect(T.pos[:, p:p + k]), T[tb][:, lo:hi], T[eb][:, lo:hi], ALU.add)],
+               [("pos", p, p + k), (tb, lo, hi), (eb, lo, hi)], [wn], ("sc", hi - lo), tag="scat%d_%d" % (t, lo))
+
+        backs, scats = runs(pl["back"]), runs(pl["scat"])
         p = 0
         for i, (lo, hi) in enumerate(runs(pl["front"])):
+            now["run"] = str(i)
             front(i, lo, hi)
             while backs and backs[0][1] <= hi:
                 a, b = backs.pop(0)
-                back(i, a, b, p)
-                p += ((b - a) // 16 + 1) // 2 * 2
+                back(i, a, b, p + (a - scats[0][0]) // 16)
+                if b == scats[0][1]:
+                    scatter(*scats[0], p)
+                    p += ((b - scats.pop(0)[0]) // 16 + 1) // 2 * 2
 
         def send(e):
-            tr = []
-            for (c, r), (m, n) in zip(hands, om):
-                rid, pid = topo.addr(c, core)
-                tr.append(RemoteDMATransfer(dst_ids=[DstId(rid=rid, pnc=pid)], dma_engine_mask=m, remote_sem=T.sem["hop%d" % t],
-                                            src=Wn[:, part(r):part(r) + CAP], dst=T["hand%d" % t][:]))
-            g.remote_dma_fused(tr, local_sem=T.sem.left)
-            tr = []
-            for k, (r, (m, n)) in enumerate(zip(direct, dm)):
-                rid, pid = topo.addr(T.cores[r], core)
-                tr.append(RemoteDMATransfer(dst_ids=[DstId(rid=rid, pnc=pid)], dma_engine_mask=m,
-                                            remote_sem=T.sem[("dir%d" if k else "soon%d") % t],
-                                            src=Wn[:, part(r):part(r) + CAP], dst=T[nb][:, me * CAP:(me + 1) * CAP]))
-            g.remote_dma_fused(tr, local_sem=T.sem.left)
+            go = ([(T.cores[r], r, way_of(t, k), T[nb][:, me * CAP:(me + 1) * CAP]) for k, r in enumerate(direct)]
+                  + [(c, r, "hop", T["hand%d" % t][:]) for c, r in hands])
+            for call in plan["calls"][t]:
+                tr = []
+                for k in call:
+                    c, r, w, dst = go[k]
+                    rid, pid = topo.addr(c, core)
+                    tr.append(RemoteDMATransfer(dst_ids=[DstId(rid=rid, pnc=pid)], dma_engine_mask=sm[k][0],
+                                                remote_sem=T.sem["%s%d" % (w, t)], src=Wn[:, part(r):part(r) + CAP], dst=dst))
+                g.remote_dma_fused(tr, local_sem=T.sem.left)
             return []
         sent = op("G", send, [wn], [], ("c", 500), tag="send%d" % t)
         ops[-1]["sends"] = t
@@ -324,9 +371,10 @@ def make_ops(g, core, T, topo, me, plan):
 
     for t in range(RO):
         ply(t)
+    way = arrivals(T, topo, me, RO - 1)
     op("Y", lambda e: [g.sync.dma_start(T.y[:], T["brd%d" % RO][:])], ["brd%d" % RO], [], ("d", "small"),
        [("%s%d" % (w, RO - 1), way[w][0], w, RO - 1) for w in way], "store", own="sty")
-    return ops, RO * sum(n for m, n in dm + om)
+    return ops, left[0]
 
 
 def depend(ops):
@@ -337,17 +385,19 @@ def depend(ops):
         for a, isw in acc:
             for j, (b, lo, hi), jw in seen.get(a[0], []):
                 meet = lo < a[2] and a[1] < hi and (isw or jw)
-                if b in BANKS and o["eng"] == "P" == ops[j]["eng"]:
-                    if meet and not o["join"]:
-                        dep[j] = True
-                    dep.setdefault(j, False)
-                elif meet or b in BANKS:
-                    dep[j] = True
+                if meet and not (o["join"] and b in BANKS and ops[j]["eng"] == "P"):
+                    dep[j] = 2
+                elif b in BANKS and (o["eng"] != ops[j]["eng"] or o["eng"] in "PF"):
+                    dep[j] = max(dep.get(j, 0), 1)
         if o["behind"] is not None:
-            dep.setdefault(o["behind"], False)
+            dep.setdefault(o["behind"], 0)
         o["dep"] = dep
         for a, isw in acc:
             seen.setdefault(a[0], []).append((i, a, isw))
+
+
+def waits(before, eng, kind):
+    return kind == 2 or (kind == 1 and (before["eng"] != eng or eng == "F"))
 
 
 def span(o, c):
@@ -377,13 +427,13 @@ def arrange(ops, c, look):
     for i in range(n - 1, -1, -1):
         rank[i] += sp[i][1]
         for j, wt in ops[i]["dep"].items():
-            rank[j] = max(rank[j], rank[i] + c["sem"] if wt else rank[i] - sp[j][1] + sp[j][0])
+            rank[j] = max(rank[j], rank[i] + c["sem"] if waits(ops[j], ops[i]["eng"], wt) else rank[i] - sp[j][1] + sp[j][0])
         for e in ops[i]["ext"]:
-            rank[sent[e[3]]] = max(rank[sent[e[3]]], rank[i] + c[e[2]])
+            rank[sent[e[3]]] = max(rank[sent[e[3]]], rank[i] + c["come"][e[3]][e[2]])
     end, start = [None] * n, [None] * n
     busy = {e: [] for e in "SVPGY"}
     missing = [len(p) for p in pre]
-    ready = {i: 0.0 for i in range(n) if not pre[i]}
+    ready = [i for i in range(n) if not pre[i]]
 
     def gap(e, s, d):
         for a, b in busy[e]:
@@ -391,21 +441,24 @@ def arrange(ops, c, look):
                 break
             s = max(s, b)
         return s
+
+    def soonest(i, e):
+        s = max([0.0] + [end[j] + c["sem"] if waits(ops[j], e, wt) else start[j] + sp[j][0] for j, wt in ops[i]["dep"].items()]
+                + [start[sent[x[3]]] + c["come"][x[3]][x[2]] for x in ops[i]["ext"]])
+        return gap(e, s, sp[i][0]) - (look if e == "S" else 0.0), e
     while ready:
-        i = max(ready, key=lambda z: rank[z] - (c["yield"] if ops[z]["cost"][0] == "ga" else 0.0))
+        i = max(ready, key=lambda z: rank[z] + ops[z]["bias"])
         o = ops[i]
-        s, e = min((gap(e, ready[i], sp[i][0]), e) for e in ("SV" if o["eng"] == "F" else o["eng"]))
-        if o["eng"] == "F" and gap("S", ready[i], sp[i][0]) <= s + look:
-            s, e = gap("S", ready[i], sp[i][0]), "S"
+        s, e = min(soonest(i, e) for e in ("SV" if o["eng"] == "F" else o["eng"]))
+        s += look if e == "S" else 0.0
         o["eng"] = e
         start[i], end[i] = s, s + sp[i][1]
         busy[e] = sorted(busy[e] + [(s, s + sp[i][0])])
-        del ready[i]
+        ready.remove(i)
         for k in post[i]:
             missing[k] -= 1
             if not missing[k]:
-                ready[k] = max([end[j] + c["sem"] if wt else start[j] + sp[j][0] for j, wt in ops[k]["dep"].items()]
-                               + [start[sent[e[3]]] + c[e[2]] + (c["first"] if e[3] == 0 else 0.0) for e in ops[k]["ext"]])
+                ready.append(k)
     return sorted(range(n), key=lambda z: (start[z], z)), start, end
 
 
@@ -421,7 +474,7 @@ def emit(g, T, ops, order, left):
         e = o["eng"]
         need = {}
         for j, wt in o["dep"].items():
-            if wt and j in mark:
+            if waits(ops[j], e, wt) and j in mark:
                 s, v = mark[j]
                 need[s] = max(need.get(s, 0), v)
         for x in o["ext"]:
@@ -457,12 +510,13 @@ def helper_program(g, core, T, topo):
             if c != core:
                 continue
             rid, pid = topo.addr(T.cores[r], core)
-            _, om, hm = masks(T, topo, a)
+            k = len(routes(T, topo, a)[0]) + i
             for t in range(RO):
-                g.wait_ge(T.sem["hop%d" % t], om[i][1])
-                g.remote_dma(T["brd%d" % (t + 1)][:, a * CAP:(a + 1) * CAP], T["hand%d" % t][:], T.sem["far%d" % t], T.sem.left,
-                             pid, rid, hm[i][0])
-            g.wait_ge(T.sem.left, RO * hm[i][1])
+                first, second = masks(T, topo, a, t)
+                g.wait_ge(T.sem["hop%d" % t], first[k][1])
+                g.remote_dma(T["brd%d" % (t + 1)][:, a * CAP:(a + 1) * CAP], T["hand%d" % t][:], T.sem["%s%d" % (way_of(t, k), t)],
+                             T.sem.left, pid, rid, second[i][0])
+            g.wait_ge(T.sem.left, RO * second[i][1])
 
 
 def rank_program(g, core, T, topo):

from concourse.bass import DstId, RemoteDMATransfer
from concourse.mybir import AluOpType as ALU, ActivationFunctionType as ACT

N, S, CAP, W, RO = 8, 384, 48, 4096, 3
K = 136
STRIDE = S
SPARE = S + 16
MID = N // 2 * STRIDE
WIN = N * STRIDE + SPARE
BIG = 32768.0
WSUM = 1365

SCRATCH = {"pol16": ("sbuf", [128, 128], "float16"), "wd": ("sbuf", [128, 144], "float16"), "init": ("sbuf", [128, 4], "float32"),
           "ddx": ("sbuf", [128, 144], "bfloat16"), "step": ("sbuf", [128, S // 2], "bfloat16"),
           "rows": ("sbuf", [128, 392], "float32"), "mrow": ("sbuf", [128, 32], "bfloat16"), "wd0": ("sbuf", [128, 144], "bfloat16"),
           "lutb": ("sbuf", [128, W], "bfloat16"), "gat": ("sbuf", [128, 16 * S], "bfloat16"), "qq": ("sbuf", [128, S + 16], "bfloat16"),
           "pos": ("sbuf", [128, 48], "uint16")}
for _n in ("plb", "pl2", "polb", "ones", "ident", "ibig", "ibig2", "bt", "both"):
    SCRATCH[_n] = ("sbuf", [128, 128], "bfloat16")
for _n, _d in (("num", "uint16"), ("relu", "float16"), ("tt", "bfloat16"), ("ee", "bfloat16"), ("t0", "bfloat16"), ("cum", "float32"),
               ("val", "float16"), ("xm", "bfloat16"), ("e0", "bfloat16")):
    SCRATCH[_n] = ("sbuf", [128, S], _d)
for _t in range(RO + 1):
    SCRATCH["brd%d" % _t] = ("sbuf", [128, S], "bfloat16")
for _t in range(RO):
    SCRATCH["win%d" % _t] = ("sbuf", [128, WIN], "bfloat16")
    SCRATCH["hand%d" % _t] = ("sbuf", [128, CAP], "bfloat16")
BANKS = tuple("bank%d" % _b for _b in range(8))
PAIRS = (BANKS[0:2], BANKS[2:4], BANKS[6:8])
for _n in BANKS:
    SCRATCH[_n] = ("psum", [128, 512], "float32")

SEMAPHORES = ["cv", "cs", "cp", "cg", "ldx", "ldpl", "ldpol", "ldlut", "sty", "left"]
WAYS = ("da", "db", "dc", "dd", "far")
for _t in range(RO):
    SEMAPHORES += ["%s%d" % (_w, _t) for _w in WAYS + ("hop",)]

PLAN = {"first": {"gat": [72, 72, 72, 72, 56, 40], "conv": [4, 4], "h": [144, 144, 96], "front": [144, 144, 96],
                  "back": [144, 144, 96], "scat": [144, 144, 96], "bias": {}},
        "later": {"gat": [24] * 4 + [48] * 4 + [32, 32, 16, 16], "conv": [2, 2, 2], "h": [96, 96, 96, 48, 48], "front": [3, 1],
                  "back": [3], "scat": [3], "bias": {"relu2": 400.0}},
        "second": {"gat": [24] * 4 + [48, 48, 40, 56, 40, 56], "conv": [2, 2], "h": [48, 144, 96, 96], "front": [3, 2],
                   "back": [2], "scat": [2], "bias": {}},
        "early": [[[0], [1, 2]], [[0]], []],
        "calls": [[[3, 4, 5, 6], [0], [1, 2]]] * RO, "helpers": [2, 3, 0, 1],
        "cast": "F", "look": 0.0, "piece": 4}
COST = {"f": 1.05, "gam": 1.56, "sig": 3.0, "pe": 0.3, "mm": 60, "sem": 200.0, "load": 3400.0, "pol": 4600.0, "small": 1600.0,
        "come": [{"da": 2300.0, "db": 3400.0, "far": 4600.0}, {"da": 1500.0, "far": 3000.0}, {"far": 3000.0}]}


def routes(T, topo, a):
    src = T.cores[a]
    ring = [(a + k) % N for k in range(1, N)]
    direct = [r for r in ring if topo.may_write(src, T.cores[r])]
    far = [r for r in ring if r not in direct]
    helpers = [c for c in topo.cores_of(src) if T.rank_of(c) is None and all(topo.may_write(c, T.cores[r]) for r in far)]
    helpers.sort(key=lambda c: topo.die(c) != topo.die(src))
    return direct, list(zip([helpers[k] for k in PLAN["helpers"]], far))


def shares(engines, n):
    sizes = [1] * n
    while sum(sizes) + min(sizes) <= len(engines):
        sizes[sizes.index(min(sizes))] *= 2
    out, p = [], 0
    for s in sorted(sizes, reverse=True):
        out.append((sum(1 << e for e in engines[p:p + s]), s))
        p += s
    return out


def masks(T, topo, a, t):
    src = T.cores[a]
    direct, hands = routes(T, topo, a)
    off = topo.engines(src, T.cores[direct[0]])
    on = topo.engines(src, hands[0][0])
    out = {}
    for call in PLAN["calls"][t]:
        away, here = [k for k in call if k < len(direct)], [k for k in call if k >= len(direct)]
        out.update(zip(away, shares(off, len(away)) if away else []))
        out.update(zip(here, shares([e for e in on if not away or e not in off], len(here)) if here else []))
    return [out[k] for k in range(N - 1)], [shares(topo.engines(h, T.cores[r]), 1)[0] for h, r in hands]


def way_of(t, k):
    return ([w for w, z in zip(WAYS, PLAN["early"][t]) if k in z] + [WAYS[-1]])[0]


def arrivals(T, topo, me, t):
    way = {w: [0, []] for w in WAYS[:len(PLAN["early"][t])] + WAYS[-1:]}
    for a in range(N):
        if a == me:
            continue
        direct, hands = routes(T, topo, a)
        first, second = masks(T, topo, a, t)
        k = (direct + [r for h, r in hands]).index(me)
        way[way_of(t, k)][0] += (first[:len(direct)] + second)[k][1]
        way[way_of(t, k)][1].append(a)
    return way


def runs(sizes, p=0):
    out = []
    for n in sizes:
        out.append((p, p + n))
        p += n
    return out


def part(r):
    return r * STRIDE + (SPARE if r * STRIDE >= MID else 0)


def make_ops(g, core, T, topo, me, plan):
    ops = []
    now = {"bias": {}, "run": ""}
    V, A, P = g.vector, g.scalar, g.tensor

    def op(eng, fn, reads=(), writes=(), cost=("c", 64), ext=(), tag="", join=False, own=None, behind=None):
        ops.append({"eng": eng, "fn": fn, "r": [whole(a) for a in reads], "w": [whole(a) for a in writes], "cost": cost,
                    "ext": list(ext), "tag": tag, "join": join, "own": own, "behind": behind,
                    "bias": now["bias"].get(tag.rstrip("0123456789_") + now["run"], 0.0)})
        return len(ops) - 1

    def whole(a):
        return (a, 0, 1 << 20) if isinstance(a, str) else a

    def ts(out, in0, s1, s2, o0, o1=None):
        if o1 is None:
            return [V.tensor_scalar(out, in0, s1, None, o0)]
        return [V.tensor_scalar(out, in0, s1, s2, o0, o1)]

    def fill(name, value, cols=slice(None), n=64):
        op("V", lambda e: [V.memset(T[name][:, cols], value)], [], [name], ("c", n))

    def select(name, pattern, cmp, base, cm, cols=slice(0, 128), put=0.0):
        op("G", lambda e: [g.affine_select(T[name][:, cols], T[name][:, cols], pattern, cmp, put, base, cm)], [name], [name],
           ("g", cols.stop - cols.start))

    def count(out, pattern, base, name, n, reads=(), behind=None):
        op("G", lambda e: [g.iota(out, pattern, base, 0, allow_small_or_imprecise_dtypes=True)], reads, [name], ("g", n),
           behind=behind)

    def affine(out, src, scale, add, reads, writes, n, relu=False, tag="", eng="F"):
        def fn(e):
            if e == "S":
                return [A.activation(out, src, ACT.Relu if relu else ACT.Identity, add, scale)]
            if relu:
                return ts(out, src, add, 0.0, ALU.add, ALU.max)
            return ts(out, src, scale, add, ALU.mult, ALU.add)
        op(eng, fn, reads, writes, ("c", n), tag=tag)

    def mm(steps, reads, writes, tag="", ext=(), start=True, stop=True):
        def fn(e):
            out = [P.matmul(o, l, r, start and i == 0, stop and i == len(steps) - 1) for i, (o, l, r, n) in enumerate(steps)]
            return out[-1:] if stop else []
        op("P", fn, reads, writes, ("p", sum(COST["mm"] + max(64, z[3]) for z in steps)), ext, tag, join=not start)

    def load(queue, name, src, cost, sem, behind=None):
        q = {"S": A, "Y": g.sync}[queue]
        return op(queue, lambda e: [q.dma_start(T[name][:], src[:])], [], [name], ("d", cost), own=sem, behind=behind)
    load("S", "brd0", T.x, "small", "ldx")
    i = load("Y", "plb", T.pl, "small", "ldpl")
    i = load("Y", "lutb", T.lut, "load", "ldlut", i)
    load("Y", "polb", T.pol, "pol", "ldpol", i)

    fill("ident", 1.0)
    select("ident", [[-1, 128]], ALU.is_equal, 0, 1)
    affine(T.ibig[:], T.ident[:], BIG, 0.0, ["ident"], ["ibig"], 128)
    affine(T.ibig2[:], T.ident[:], 2 * BIG, 0.0, ["ident"], ["ibig2"], 128)
    affine(T.pl2[:], T.plb[:], 2.0, 0.0, ["plb"], ["pl2"], 128)
    affine(T.pol16[:], T.polb[:], 1.0, 0.0, ["polb"], ["pol16"], 128)
    fill("bt", 0.25)
    select("bt", [[0, 8], [-1, 16]], ALU.is_ge, N, 0)
    select("bt", [[-16, 8], [0, 16]], ALU.is_ge, 0, 1)
    select("bt", [[16, 8], [0, 16]], ALU.is_ge, 15, -1)
    fill("ones", 1.0)
    fill("rows", 1.0, slice(384, 392))
    count(T.rows[0:1, 0:128], [[0, 8], [1, 16]], 0, ("rows", 0, 128), 128)
    count(T.rows[0:1, 128:256], [[2, 8], [1, 16]], MID, ("rows", 128, 256), 128)
    count(T.rows[0:1, 256:384], [[-1, 16], [MID + SPARE, 2], [STRIDE, N // 2]], 1 - MID, ("rows", 256, 384), 128)
    count(T.mrow[0:1, :], [[16, 32]], 0, "mrow", 32)
    for j in range(3):
        mm([(T.bank7[:, j:j + 1], T.rows[0:1, 128 * j:128 * j + 128], T.rows[0:1, 384:385], 256)], ["rows"], [("bank7", j, j + 1)])
    affine(T.init[:, 0:1], T.bank7[:, 0:1], -0.125, -K - 0.4375, ["bank7"], ["init"], 64)
    affine(T.init[:, 1:3], T.bank7[:, 1:3], 1.0, 0.0, ["bank7"], ["init"], 64)
    fill("step", -2.0)
    fill("ddx", 0.0)
    select("ddx", [[-1, 128]], ALU.not_equal, 0, 1, slice(8, 136), 1.0)
    select("ddx", [[-1, 128]], ALU.not_equal, -1, 1, slice(8, 136), -1.0)
    select("ddx", [[0, 8], [-1, 16]], ALU.is_ge, N - 1, 0, slice(8, 136))
    same = [T.ddx[:, 8:136], T.ddx[:, 0:128]]
    op("V", lambda e: [V.tensor_tensor(T.both[:], same[0], same[1], ALU.add)], ["ddx"], ["both"], ("c", 256))
    earlier = [(T.both[:], 0), (same[1], 1), (same[0], -1)]
    fill("wd0", 0.0)
    fill("wd0", 1.0, slice(14, 144, 16))
    fill("wd0", 1.0, slice(15, 144, 16))
    select("wd0", [[-16, 9], [-8, 16]], ALU.is_ge, 112, 1, slice(0, 144))
    select("wd0", [[16, 9], [8, 16]], ALU.is_ge, 7 - 112, -1, slice(0, 144))
    affine(T.wd[:], T.wd0[:], 1.0, 0.0, ["wd0"], ["wd"], 144)
    fill("qq", 0.0, slice(0, 8))

    op("V", lambda e: ts(T.xm[:], T.brd0[:], 0.0, float(K), ALU.is_ge, ALU.mult), ["brd0"], ["xm"], ("c", S // 2))

    def clear(t, behind):
        wn = "win%d" % t
        for p in map(part, range(N)):
            count(T[wn][:, p:p + CAP], [[0, CAP]], -1 if t == RO - 1 else 0, (wn, p, p + CAP), CAP, ["wd0"], behind)
    clear(0, None)

    direct, hands = routes(T, topo, me)
    left = [0]

    def ply(t):
        way = arrivals(T, topo, me, t - 1)
        sm = masks(T, topo, me, t)[0]
        left[0] += sum(n for m, n in sm)
        pl = plan["first"] if t == 0 else dict(plan["later"], **(plan["second"] if t == 1 else {}))
        last, kt = t == RO - 1, K + 2 * t
        pw, big = ("pl2", "ibig2") if t else ("plb", "ibig")
        now.update(bias=pl["bias"], run="")
        bn, wn, nb = "brd%d" % t, "win%d" % t, "brd%d" % (t + 1)
        B, Wn = T[bn], T[wn]
        if t == 0:
            lots = [(None, list(range(a, b))) for a, b in runs(pl["conv"])]
        else:
            late = sorted(way["far"][1])
            lots = ([(None, [me])] + [(w, sorted(way[w][1])) for w in way if w != "far"]
                    + [("far", late[a:b]) for a, b in runs(pl["conv"]) if late[a:b]])
            pl = dict(pl)
            for z in ("front", "back", "scat"):
                cut = [0] + [CAP * late[-k] for k in pl[z]] + [S]
                pl[z] = [b - a for a, b in zip(cut, cut[1:])]
        order = [a for w, blocks in lots for a in blocks]

        def pieces(lo, hi):
            out = []
            for s in range(lo, hi):
                c = order.index(s // CAP) * CAP + s % CAP
                if out and out[-1][1] + out[-1][2] == c:
                    out[-1][2] += 1
                else:
                    out.append([s, c, 1])
            return sorted(out, key=lambda z: z[1])

        def gather(c, n):
            def fn(e):
                src = T.lutb[:, 0:W].indirect(T.num[:, c:c + n])
                if e == "V":
                    return [V.tensor_copy(T.gat[:, 16 * c:16 * (c + n)], src)]
                return [A.activation(T.gat[:, 16 * c:16 * (c + n)], src, ACT.Copy)]
            op("F", fn, ["lutb", ("num", c, c + n)], [("gat", c, c + n)], ("ga", 16 * n), tag="gat%d_%d" % (t, c))

        def hsum(i, a, b):
            bk, pc = BANKS[4 + i % 2], plan["piece"]
            for j0 in range(0, 16, pc):
                mm([(T[bk][:, 0:b - a], T.ident[:], T.gat[:, 16 * a + j:16 * b:16], b - a) for j in range(j0, j0 + pc)],
                   ["ident", ("gat", a, b)], [(bk, 0, b - a)], "h%d_%d" % (t, a), start=j0 == 0, stop=j0 + pc == 16)
            affine(T.relu[:, a:b], T[bk][:, 0:b - a], 1.0, 0.0, [(bk, 0, b - a)], [("relu", a, b)], b - a, True, "relu%d_%d" % (t, a))

        def arrived(blocks):
            return [("%s%d" % (w, t - 1), way[w][0], w, t - 1) for w in way if t > 0 and any(a in way[w][1] for a in blocks)]

        col = 0
        for i, (w, blocks) in enumerate(lots):
            bk = BANKS[6 + i % 2]
            spans = []
            for j, a in enumerate(blocks):
                if spans and spans[-1][1] + spans[-1][2] == a * CAP:
                    spans[-1][2] += CAP
                else:
                    spans.append([j * CAP, a * CAP, CAP])
            n = CAP * len(blocks)
            op("P", lambda e, bk=bk, spans=spans: [P.matmul(T[bk][:, c:c + m], T[pw][:], B[:, k:k + m], True, True)
                                                   for c, k, m in spans][-1:],
               [pw] + [(bn, k, k + m) for c, k, m in spans], [(bk, 0, n)], ("p", sum(COST["mm"] + max(64, m) for c, k, m in spans)),
               arrived(blocks), "num%d" % t)
            affine(T.num[:, col:col + n], T[bk][:, 0:n], 1.0, -float(kt * WSUM) if t else 0.0, [(bk, 0, n)], [("num", col, col + n)],
                   n, True, "conv%d" % t, plan["cast"])
            col += n
        for (a, b), eng in zip(runs(pl["gat"]), pl.get("by", "F" * S)):
            gather(a, b - a)
            ops[-1]["eng"] = eng
        for i, (a, b) in enumerate(runs(pl["h"])):
            now["run"] = str(i)
            hsum(i, a, b)

        def front(i, lo, hi):
            n = hi - lo
            pa, pb = PAIRS[i]
            terms = [bn] if t else [bn, "xm"]
            mm([(T[pb][:, 0:n], T[big][:], T[z][:, lo:hi], n) for z in terms], [big] + [(z, lo, hi) for z in terms],
               [(pb, 0, n)], "zb%d" % t, arrived(range(lo // CAP, (hi - 1) // CAP + 1)), stop=False)
            todo = pieces(lo, hi)
            for s, c, m in todo:
                mm([(T[pb][:, s - lo:s - lo + m], T.pol16[:], T.relu[:, c:c + m], m)], ["pol16", ("relu", c, c + m)],
                   [(pb, s - lo, s - lo + m)], "z%d" % t, start=False, stop=s == todo[-1][0])
            half, wrap = 0.25 - 0.25 / BIG, (kt + 3) * BIG + 0.5

            def grow(e):
                if e == "S":
                    return [A.activation(T.tt[:, lo:hi], T[pb][:, 0:n], ACT.Identity, half, 0.5 / BIG),
                            A.activation(T.ee[:, lo:hi], T[pb][:, 0:n], ACT.Sign, wrap, -1.0)]
                return (ts(T.tt[:, lo:hi], T[pb][:, 0:n], 0.5 / BIG, half + 1, ALU.mult, ALU.add)
                        + ts(T.ee[:, lo:hi], T[pb][:, 0:n], wrap, -2.0, ALU.is_ge, ALU.mult))
            op("F", grow, [(pb, 0, n)], [("tt", lo, hi), ("ee", lo, hi)], ("c", 2 * max(n, 64) + 40), tag="te%d_%d" % (t, lo))
            mm([(T[pa][:, 0:n], T.bt[:], T.tt[:, lo:hi], n), (T[pa][:, 0:n], T.bt[:], T.ee[:, lo:hi], n)],
               ["bt", ("tt", lo, hi), ("ee", lo, hi)], [(pa, 0, n)], "u%d" % t)
            affine(T.qq[:, 8 + lo:8 + hi], T[pa][:, 0:n], 1.0, T.init[:, 0:1], ["init", (pa, 0, n)], [("qq", 8 + lo, 8 + hi)], n, True,
                   "q%d_%d" % (t, lo))
            if last:
                affine(T.t0[:, lo:hi], T.tt[:, lo:hi], 2.0, -kt - 2.0, [("tt", lo, hi)], [("t0", lo, hi)], n, tag="t0_%d" % lo)
                affine(T.e0[:, lo:hi], T.ee[:, lo:hi], 2.0, 0.0, [("ee", lo, hi)], [("e0", lo, hi)], n, tag="e0_%d" % lo)

        def back(i, lo, hi, p):
            n, k, a, b = hi - lo, (hi - lo) // 16, lo // 2, hi // 2
            m = b - a
            pa, pb = PAIRS[i]
            mm([(T[pb][:, 0:m], w, T.qq[:, 8 + lo + d:8 + hi + d:2], m) for w, d in earlier],
               ["both", "ddx", ("qq", 7 + lo, 8 + hi)], [(pb, 0, m)], "cnt%d" % t)
            mm([(T[pa][:, 0:m], same[d], T.qq[:, 8 + lo + d:8 + hi:2], m) for d in range(2)], ["ddx", ("qq", 8 + lo, 8 + hi)],
               [(pa, 0, m)], "ind%d" % t)
            first = T.init[:, 2:3] if lo == 0 else T.cum[:, a - 1:a]
            op("V", lambda e: [V.tensor_tensor_scan(T.cum[:, a:b], T[pb][:, 0:m], T.step[:, a:b], first, ALU.add, ALU.add)],
               [(pb, 0, m), "step", "init", ("cum", max(a - 1, 0), a)], [("cum", a, b)], ("c", m), tag="scan%d_%d" % (t, lo))
            op("V", lambda e: [V.tensor_tensor(T.val[:, a:b], T[pa][:, 0:m], T.cum[:, a:b], ALU.mult)],
               [(pa, 0, m), ("cum", a, b)], [("val", a, b)], ("c", m), tag="val%d_%d" % (t, lo))
            mm([(T[pb][:, 0:k], T.ones[0:1, :], T.mrow[0:1, lo // 16:hi // 16], k)], ["ones", "mrow"], [(pb, 0, k)],
               "spare%d" % t, stop=False)
            mm([(T[pb][:, 0:k], T.wd[:, 14 - 2 * j:142 - 2 * j], T.val[:, a + j:b:8], k) for j in range(8)], ["wd", ("val", a, b)],
               [(pb, 0, k)], "wrap%d" % t, start=False)
            affine(T.pos[:, p:p + k], T[pb][:, 0:k], 1.0, T.init[:, 1:2], [(pb, 0, k), "init"], [("pos", p, p + k)], k, True,
                   "pos%d_%d" % (t, lo), plan["cast"])

        def scatter(lo, hi, p):
            (tb, eb), k = ("t0", "e0") if last else ("tt", "ee"), (hi - lo) // 16
            op("V", lambda e: [V.tensor_tensor(Wn[:, 0:WIN].indirect(T.pos[:, p:p + k]), T[tb][:, lo:hi], T[eb][:, lo:hi], ALU.add)],
               [("pos", p, p + k), (tb, lo, hi), (eb, lo, hi)], [wn], ("sc", hi - lo), tag="scat%d_%d" % (t, lo))

        backs, scats = runs(pl["back"]), runs(pl["scat"])
        p = 0
        for i, (lo, hi) in enumerate(runs(pl["front"])):
            now["run"] = str(i)
            front(i, lo, hi)
            while backs and backs[0][1] <= hi:
                a, b = backs.pop(0)
                back(i, a, b, p + (a - scats[0][0]) // 16)
                if b == scats[0][1]:
                    scatter(*scats[0], p)
                    p += ((b - scats.pop(0)[0]) // 16 + 1) // 2 * 2

        def send(e):
            go = ([(T.cores[r], r, way_of(t, k), T[nb][:, me * CAP:(me + 1) * CAP]) for k, r in enumerate(direct)]
                  + [(c, r, "hop", T["hand%d" % t][:]) for c, r in hands])
            for call in plan["calls"][t]:
                tr = []
                for k in call:
                    c, r, w, dst = go[k]
                    rid, pid = topo.addr(c, core)
                    tr.append(RemoteDMATransfer(dst_ids=[DstId(rid=rid, pnc=pid)], dma_engine_mask=sm[k][0],
                                                remote_sem=T.sem["%s%d" % (w, t)], src=Wn[:, part(r):part(r) + CAP], dst=dst))
                g.remote_dma_fused(tr, local_sem=T.sem.left)
            return []
        sent = op("G", send, [wn], [], ("c", 500), tag="send%d" % t)
        ops[-1]["sends"] = t
        p = part(me)
        affine(T[nb][:, me * CAP:(me + 1) * CAP], Wn[:, p:p + CAP], 1.0, 0.0, [(wn, p, p + CAP)], [(nb, me * CAP, (me + 1) * CAP)],
               CAP, tag="own%d" % t)
        if not last:
            clear(t + 1, sent)

    for t in range(RO):
        ply(t)
    way = arrivals(T, topo, me, RO - 1)
    op("Y", lambda e: [g.sync.dma_start(T.y[:], T["brd%d" % RO][:])], ["brd%d" % RO], [], ("d", "small"),
       [("%s%d" % (w, RO - 1), way[w][0], w, RO - 1) for w in way], "store", own="sty")
    return ops, left[0]


def depend(ops):
    seen = {}
    for i, o in enumerate(ops):
        dep = {}
        acc = [(a, False) for a in o["r"]] + [(a, True) for a in o["w"]]
        for a, isw in acc:
            for j, (b, lo, hi), jw in seen.get(a[0], []):
                meet = lo < a[2] and a[1] < hi and (isw or jw)
                if meet and not (o["join"] and b in BANKS and ops[j]["eng"] == "P"):
                    dep[j] = 2
                elif b in BANKS and (o["eng"] != ops[j]["eng"] or o["eng"] in "PF"):
                    dep[j] = max(dep.get(j, 0), 1)
        if o["behind"] is not None:
            dep.setdefault(o["behind"], 0)
        o["dep"] = dep
        for a, isw in acc:
            seen.setdefault(a[0], []).append((i, a, isw))


def waits(before, eng, kind):
    return kind == 2 or (kind == 1 and (before["eng"] != eng or eng == "F"))


def span(o, c):
    kind, n = o["cost"]
    if kind == "d":
        return 100.0, c[n]
    cyc = 0.83 * c["f"]
    if kind == "p":
        d = 12 + n * c["pe"] * c["f"]
    elif kind == "c":
        d = 30 + max(64, n) * cyc
    else:
        d = {"g": 170 + 2 * n * cyc, "ga": 60 + n * c["gam"] * cyc, "sc": 60 + n * c["sig"] * cyc}[kind]
    return d, d


def arrange(ops, c, look):
    n = len(ops)
    sent = {o["sends"]: i for i, o in enumerate(ops) if "sends" in o}
    sp = [span(o, c) for o in ops]
    pre = [set(o["dep"]) | set(sent[e[3]] for e in o["ext"]) for o in ops]
    post = [[] for o in ops]
    for i in range(n):
        for j in pre[i]:
            post[j].append(i)
    rank = [0.0] * n
    for i in range(n - 1, -1, -1):
        rank[i] += sp[i][1]
        for j, wt in ops[i]["dep"].items():
            rank[j] = max(rank[j], rank[i] + c["sem"] if waits(ops[j], ops[i]["eng"], wt) else rank[i] - sp[j][1] + sp[j][0])
        for e in ops[i]["ext"]:
            rank[sent[e[3]]] = max(rank[sent[e[3]]], rank[i] + c["come"][e[3]][e[2]])
    end, start = [None] * n, [None] * n
    busy = {e: [] for e in "SVPGY"}
    missing = [len(p) for p in pre]
    ready = [i for i in range(n) if not pre[i]]

    def gap(e, s, d):
        for a, b in busy[e]:
            if s + d <= a:
                break
            s = max(s, b)
        return s

    def soonest(i, e):
        s = max([0.0] + [end[j] + c["sem"] if waits(ops[j], e, wt) else start[j] + sp[j][0] for j, wt in ops[i]["dep"].items()]
                + [start[sent[x[3]]] + c["come"][x[3]][x[2]] for x in ops[i]["ext"]])
        return gap(e, s, sp[i][0]) - (look if e == "S" else 0.0), e
    while ready:
        i = max(ready, key=lambda z: rank[z] + ops[z]["bias"])
        o = ops[i]
        s, e = min(soonest(i, e) for e in ("SV" if o["eng"] == "F" else o["eng"]))
        s += look if e == "S" else 0.0
        o["eng"] = e
        start[i], end[i] = s, s + sp[i][1]
        busy[e] = sorted(busy[e] + [(s, s + sp[i][0])])
        ready.remove(i)
        for k in post[i]:
            missing[k] -= 1
            if not missing[k]:
                ready.append(k)
    return sorted(range(n), key=lambda z: (start[z], z)), start, end


def emit(g, T, ops, order, left):
    queue = {"V": g.vector, "S": g.scalar, "P": g.tensor, "G": g, "Y": g.sync}
    counter = {"V": "cv", "S": "cs", "P": "cp", "G": "cg"}
    count = {}
    mark = {}
    know = {e: {} for e in queue}
    after = {}
    for i in order:
        o = ops[i]
        e = o["eng"]
        need = {}
        for j, wt in o["dep"].items():
            if waits(ops[j], e, wt) and j in mark:
                s, v = mark[j]
                need[s] = max(need.get(s, 0), v)
        for x in o["ext"]:
            need[x[0]] = x[1]
        for s, v in sorted(need.items(), key=lambda z: -len(after.get(z, {}))):
            if know[e].get(s, 0) < v:
                queue[e].wait_ge(T.sem[s], v)
                know[e][s] = v
                for s2, v2 in after.get((s, v), {}).items():
                    know[e][s2] = max(know[e].get(s2, 0), v2)
        ins = o["fn"](e)
        if o["own"]:
            ins[0].then_inc(T.sem[o["own"]], 16)
            mark[i] = (o["own"], 16)
            count[o["own"]] = 16
        elif ins:
            s = counter[e]
            for z in ins:
                z.then_inc(T.sem[s], 1)
                count[s] = count.get(s, 0) + 1
            mark[i] = (s, count[s])
        if i in mark:
            after[mark[i]] = dict(know[e])
    for s, v in count.items():
        if not any(k.get(s, 0) >= v for k in know.values()):
            (g.sync if s == "sty" else g).wait_ge(T.sem[s], v)
    g.wait_ge(T.sem.left, left)


def helper_program(g, core, T, topo):
    for a in range(N):
        for i, (c, r) in enumerate(routes(T, topo, a)[1]):
            if c != core:
                continue
            rid, pid = topo.addr(T.cores[r], core)
            k = len(routes(T, topo, a)[0]) + i
            for t in range(RO):
                first, second = masks(T, topo, a, t)
                g.wait_ge(T.sem["hop%d" % t], first[k][1])
                g.remote_dma(T["brd%d" % (t + 1)][:, a * CAP:(a + 1) * CAP], T["hand%d" % t][:], T.sem["%s%d" % (way_of(t, k), t)],
                             T.sem.left, pid, rid, second[i][0])
            g.wait_ge(T.sem.left, RO * second[i][1])


def rank_program(g, core, T, topo):
    me = T.rank_of(core)
    if me is None:
        helper_program(g, core, T, topo)
        return
    ops, left = make_ops(g, core, T, topo, me, PLAN)
    depend(ops)
    order, _, _ = arrange(ops, COST, PLAN["look"])
    emit(g, T, ops, order, left)
